import numpy as np
import ml_dtypes


def mxq(x, axis, fmt="e4m3"):
    dtype, down = {"e4m3": (ml_dtypes.float8_e4m3fn, 7), "e5m2": (ml_dtypes.float8_e5m2, 14)}[fmt]
    v = np.moveaxis(np.asarray(x, np.float32).astype(ml_dtypes.bfloat16).astype(np.float64), axis, -1)
    blocks = v.reshape(v.shape[:-1] + (-1, 32))
    amax = np.abs(blocks).max(-1, keepdims=True)
    byte = np.maximum(np.where(amax > 0, np.frexp(amax)[1] - 1 + 127, 0) - down, 1)
    scale = np.exp2(byte - 127.0)
    codes = (blocks / scale).astype(np.float32).astype(dtype).astype(np.float64)
    return np.moveaxis((codes * scale).reshape(v.shape), -1, axis)


WIDE = False


def mx_kscale(k):
    if not WIDE:
        return np.ones(k)
    levels = np.array([10, -10, 5, -5, 0])
    if k % 512:
        return np.exp2(np.random.permutation(np.resize(levels, k // 32))).repeat(32)
    a = np.empty((k // 512, 16))
    for p in range(k // 512):
        a[p, :8] = np.random.permutation(np.resize(levels, 8))
        for g in range(8):
            far = levels[np.abs(levels - a[p, g]) >= 10]
            a[p, g + 8] = far[np.random.randint(len(far))]
    return np.exp2(a.ravel()).repeat(32)


def f64(x):
    return np.asarray(x).astype(np.float64)


def striped(idx):
    return np.tile(idx.reshape(-1, 16).T, (8, 1)).astype(np.uint16)


def unstriped(offs):
    return offs[:16].T.reshape(-1).astype(np.int64)


E2M1 = np.array([0.0, 0.5, 1.0, 1.5, 2.0, 3.0, 4.0, 6.0, -0.0, -0.5, -1.0, -1.5, -2.0, -3.0, -4.0, -6.0])


def pack_weight(w, fmt):
    k, n = w.shape
    w = f64(np.asarray(w, np.float32).astype(ml_dtypes.bfloat16)).reshape(k // 32, 32, n)
    amax = np.abs(w).max(1)
    if fmt == "e4m3":
        byte = np.frexp(amax)[1] - 1 + 127 - 7
    else:
        mant, ex = np.frexp(amax / 6.0)
        byte = np.where(mant > 0.5, ex, ex - 1) + 127
    byte = np.clip(np.where(amax > 0, byte, 1), 1, 254)
    scaled = (w * np.exp2(127.0 - byte)[:, None, :]).reshape(k, n).astype(np.float32)
    by_word = np.ascontiguousarray(scaled.reshape(k // 512, 128, 4, n).transpose(0, 1, 3, 2))
    if fmt == "e4m3":
        words = by_word.astype(ml_dtypes.float8_e4m3fn).view(np.uint8)
    else:
        c = by_word.astype(ml_dtypes.float4_e2m1fn).view(np.uint8) & 0xF
        words = (c[..., 0::2] | (c[..., 1::2] << 4)).reshape(k // 512, 128, 2 * n)
    return np.ascontiguousarray(words), np.ascontiguousarray(byte.astype(np.uint8).reshape(k // 512, 16, n))


def unpack_weight(words, scales, fmt):
    g, _, n = scales.shape
    words = np.ascontiguousarray(words).reshape(g, 128, n, -1)
    if fmt == "e4m3":
        vals = words.view(ml_dtypes.float8_e4m3fn).astype(np.float64)
    else:
        nib = np.empty((g, 128, n, 4), np.uint8)
        nib[..., 0::2] = words & 0xF
        nib[..., 1::2] = words >> 4
        vals = E2M1[nib]
    vals = vals * np.repeat(np.exp2(scales.astype(np.float64) - 127.0), 8, axis=1)[..., None]
    return vals.transpose(0, 1, 3, 2).reshape(g * 512, n)


def silu(v):
    return v / (1.0 + np.exp(-np.maximum(v, -700.0)))


K, T, E, C, H, HS, N = 512, 512, 6, 256, 512, 512, 512
TOP = 3


def by_expert(wq, xq):
    return np.concatenate([wq[e].T @ xq[:, e * C:(e + 1) * C] for e in range(E)], axis=1)


def setup_inputs():
    n = np.random.standard_normal
    s = mx_kscale(K)
    u = mx_kscale(H)
    v = mx_kscale(HS)
    deal = np.repeat(np.arange(E), C).reshape(TOP, T)[:, np.random.permutation(T)]
    deal = np.take_along_axis(deal, np.argsort(np.random.rand(TOP, T), axis=0), axis=0)
    for _ in range(8):
        s_, t_ = np.random.permutation(T).reshape(2, -1); r = np.random.randint(TOP, size=T // 2); x, y = deal[r, s_].copy(), deal[r, t_].copy()
        ok = ~((deal[:, s_] == y).any(0) | (deal[:, t_] == x).any(0)); deal[r[ok], s_[ok]] = y[ok]; deal[r[ok], t_[ok]] = x[ok]
    order = np.lexsort((np.random.rand(TOP * T), deal.reshape(-1)))
    slot_token = order % T; pos = np.empty(TOP * T, np.int64); pos[order] = np.arange(TOP * T); pos = pos.reshape(TOP, T)
    g = np.random.uniform(0.5, 1.5, (TOP, T)); g = g / g.sum(0)
    x = pack_weight(n((K, T)) * s[:, None], "e4m3")
    w1 = [pack_weight(m, "e2m1") for m in n((E, K, H)) / np.sqrt(K) / s[None, :, None] * u]
    w2 = [pack_weight(m, "e2m1") for m in n((E, H, N)) / np.sqrt(H) / u[None, :, None]]
    w1s = pack_weight(n((K, HS)) / np.sqrt(K) / s[:, None] * v, "e4m3")
    w2s = pack_weight(n((HS, N)) / np.sqrt(HS) / v[:, None], "e4m3")
    return {
        "x_words": x[0],
        "x_scales": x[1],
        "w1_words": np.stack([m[0] for m in w1]),
        "w1_scales": np.stack([m[1] for m in w1]),
        "w2_words": np.stack([m[0] for m in w2]),
        "w2_scales": np.stack([m[1] for m in w2]),
        "w1s_words": w1s[0],
        "w1s_scales": w1s[1],
        "w2s_words": w2s[0],
        "w2s_scales": w2s[1],
        "gate": np.stack([np.tile(r, (128, 1)) for r in g]).astype(np.float32),
        "offs": striped(slot_token),
        "pos1": striped(pos[0]),
        "pos2": striped(pos[1]),
        "pos3": striped(pos[2]),
    }


def reference(x_words, x_scales, w1_words, w1_scales, w2_words, w2_scales, w1s_words, w1s_scales, w2s_words, w2s_scales, gate, offs, pos1, pos2, pos3):
    w1 = np.stack([unpack_weight(w1_words[e], w1_scales[e], "e2m1") for e in range(E)])
    w2 = np.stack([unpack_weight(w2_words[e], w2_scales[e], "e2m1") for e in range(E)])
    w1s = unpack_weight(w1s_words, w1s_scales, "e4m3")
    w2s = unpack_weight(w2s_words, w2s_scales, "e4m3")
    idx = unstriped(offs)
    x = unpack_weight(x_words, x_scales, "e4m3")
    hs = silu(w1s.T @ x)
    ys = w2s.T @ mxq(hs, 0, "e4m3")
    h = silu(by_expert(w1, x[:, idx]))
    y = by_expert(w2, mxq(h, 0, "e4m3"))
    c = sum(f64(gate[r, :1]) * y[:, unstriped(p)] for r, p in enumerate((pos1, pos2, pos3)))
    return ys + c

@@ -1,0 +1,264 @@
+from contextlib import ExitStack
+
+import concourse.mybir as mybir
+from concourse.masks import make_identity
+
+K, T, E, C, H, N, TOP = 512, 512, 6, 256, 512, 512, 3
+SLOTS = E * C
+P = 128
+FLOPS = 2 * (SLOTS + T) * (K * H + H * N)
+
+F32 = mybir.dt.float32
+BF16 = mybir.dt.bfloat16
+I32 = mybir.dt.int32
+U32 = mybir.dt.uint32
+U16 = mybir.dt.uint16
+U8 = mybir.dt.uint8
+FP8X4 = mybir.dt.float8_e4m3fn_x4
+FP4X4 = mybir.dt.float4_e2m1fn_x4
+SILU = mybir.ActivationFunctionType.Silu
+MULT = mybir.AluOpType.mult
+ADD = mybir.AluOpType.add
+
+GROUPS = [128, 128, 256, 256, 256, 256, 128, 128]
+TURN_COPY_ON_VECTOR = (3, 5, 6, 7)
+Y0_BANKS = [(0, 512), (512, 1024), (1024, 1408), (1408, 1536)]
+
+
+def tile_moe_shf_mlp_silu_kernel(
+    tc, x_words, x_scales, w1_words, w1_scales, w2_words, w2_scales,
+    w1s_words, w1s_scales, w2s_words, w2s_scales, gate, offs, pos1, pos2, pos3, out,
+):
+    nc = tc.nc
+    with ExitStack() as ctx:
+        keep = ctx.enter_context(tc.tile_pool(name="keep", bufs=1))
+        ring = ctx.enter_context(tc.tile_pool(name="ring", bufs=1))
+        psum = ctx.enter_context(tc.psum_pool(name="psum", bufs=1))
+
+        def held(shape, dtype, name):
+            return keep.tile(shape, dtype, name=name, align_bytes=64)
+
+        banks = [psum.tile([P, 512], F32, name="bank%d" % b) for b in range(8)]
+
+        offs_sb = keep.tile([P, SLOTS // 16], U16, name="offs_sb")
+        pos_sb = [keep.tile([P, T // 16], U16, name="pos_sb%d" % r) for r in range(TOP)]
+        xw = held([P, T], I32, "xw")
+        xs = held([P, T // 4], I32, "xs")
+        w1w = [held([P, 2 * H], U8, "w1w%d" % e) for e in range(E)]
+        w2w = [held([P, 2, 2 * N], U8, "w2w%d" % e) for e in range(E // 2)]
+        w1p = held([P, E, H // 4], I32, "w1p")
+        w2p = held([P, E, N // 4], I32, "w2p")
+        w1sw = held([P, H], I32, "w1sw")
+        w2sw = held([P, N], I32, "w2sw")
+        w1sp = held([P, H // 4], I32, "w1sp")
+        w2sp = held([P, N // 4], I32, "w2sp")
+        gate_sb = [held([P, T], F32, "gate_sb%d" % r) for r in range(TOP)]
+        ident = held([P, P], F32, "ident")
+        warm = held([P, 8], F32, "warm")
+
+        for plane in (w1p, w2p, w1sp, w2sp):
+            nc.vector.memset(plane[:], 0)
+        nc.gpsimd.memset(warm[:], 0.0)
+        nc.scalar.activation(warm[:], warm[:], SILU)
+        make_identity(nc, ident[:])
+
+        def load_words(tile_ap, dram):
+            nc.sync.dma_start(tile_ap, dram[0].rearrange("p n d -> p (n d)").bitcast(I32))
+
+        def load_plane(queue, plane, dram):
+            for q in range(4):
+                queue.dma_start(plane[32 * q : 32 * q + 4, :], dram[0, 4 * q : 4 * q + 4, :].bitcast(I32))
+
+        def load_planes(queue, plane, dram):
+            for q in range(4):
+                rows = dram[:, 0, 4 * q : 4 * q + 4, :].rearrange("e r n -> r e n")
+                queue.dma_start(plane[32 * q : 32 * q + 4, :, :], rows.bitcast(I32))
+
+        nc.sync.dma_start(offs_sb[:], offs)
+        for q in range(4):
+            rows = x_scales[0, 4 * q : 4 * q + 4, :].bitcast(I32)
+            nc.sync.dma_start(xs[32 * q : 32 * q + 32, :], rows.unsqueeze(0).to_broadcast([8, 4, T // 4]))
+        load_words(xw[:], x_words)
+        nc.sync.dma_start(w1w[0][:].bitcast(I32), w1_words[0, 0].bitcast(I32))
+        load_planes(nc.sync, w1p, w1_scales)
+        for e in range(1, E):
+            nc.sync.dma_start(w1w[e][:].bitcast(I32), w1_words[e, 0].bitcast(I32))
+        load_planes(nc.sync, w2p, w2_scales)
+        for e in range(E // 2):
+            pair = w2_words[2 * e : 2 * e + 2, 0].rearrange("e p n -> p e n")
+            nc.sync.dma_start(w2w[e][:].bitcast(I32), pair.bitcast(I32))
+        load_words(w1sw[:], w1s_words)
+        load_plane(nc.sync, w1sp, w1s_scales)
+        for r, pos in enumerate((pos1, pos2, pos3)):
+            nc.sync.dma_start(pos_sb[r][:], pos)
+            nc.sync.dma_start(gate_sb[r][:], gate[r])
+        load_words(w2sw[:], w2s_words)
+        load_plane(nc.sync, w2sp, w2s_scales)
+
+        first_banks = banks[0:3]
+        turn_banks = banks[3:5]
+        y_banks = banks[5:8]
+        sum_banks = banks[0:5]
+        used = {"first": 0, "turn": 0, "y": 0, "sum": 0}
+
+        def next_bank(role, ring):
+            bank = ring[used[role] % len(ring)]
+            used[role] = used[role] + 1
+            return bank
+
+        def hidden(name, cols, x_codes, x_plane, w_codes, w_plane, copy_on_vector):
+            tiles = cols // P
+            turned = next_bank("turn", turn_banks)
+            for a in range(tiles):
+                acc = next_bank("first", first_banks)
+                nc.tensor.matmul_mx(
+                    out=acc[:], lhsT=x_codes[:, a * P : (a + 1) * P].bitcast(FP8X4),
+                    lhsT_scale=x_plane[:, a * P : (a + 1) * P], rhs=w_codes, rhs_scale=w_plane,
+                    start=True, stop=True,
+                )
+                act = held([P, H], BF16, "act_%s_%d" % (name, a))
+                nc.scalar.activation(
+                    act[:].rearrange("s (u p e) -> s u p e", u=2, e=2),
+                    acc[:].rearrange("s (p u e) -> s u p e", u=2, e=2), SILU,
+                )
+                words = act[:].bitcast(F32)
+                for u in range(2):
+                    at = (2 * a + u) * P
+                    nc.tensor.transpose(turned[:, at : at + P], words[:, u * P : (u + 1) * P], ident[:])
+            grouped = held([P, 2 * cols], F32, "grouped_" + name)
+            src = turned[:, 0 : 2 * cols].rearrange("p (a u s) -> p a s u", u=2, s=P)
+            dst = grouped[:].rearrange("p (a s u) -> p a s u", u=2, s=P)
+            if copy_on_vector:
+                nc.vector.tensor_copy(dst, src)
+            else:
+                nc.scalar.copy(dst, src)
+            codes = held([P, cols], U32, "codes_" + name)
+            plane = held([P, cols], U8, "plane_" + name)
+            nc.vector.quantize_mx(out=codes[:].bitcast(FP8X4), scales=plane[:], in_=grouped[:].bitcast(BF16))
+            return codes, plane
+
+        y_sb = [held([P, SLOTS], F32, "y_sb%d" % j) for j in range(N // P)]
+        starts = [sum(GROUPS[:g]) for g in range(len(GROUPS))]
+
+        def gather(g):
+            cols = GROUPS[g]
+            picks = offs_sb[:, starts[g] // 16 : (starts[g] + cols) // 16]
+            xg = ring.tile([P, cols], U32, name="xg", bufs=3, align_bytes=64)
+            xgp = ring.tile([P, cols], U8, name="xgp", bufs=2, align_bytes=64)
+            nc.vector.tensor_copy(xgp[:], xs[:].bitcast(U8).indirect(picks))
+            nc.vector.tensor_copy(xg[:], xw[:].bitcast(U32).indirect(picks))
+            return xg, xgp
+
+        h = []
+
+        def second(j, lo, hi):
+            bank = next_bank("y", y_banks)
+            for g, cols in enumerate(GROUPS):
+                if lo <= starts[g] < hi:
+                    e = starts[g] // C
+                    nc.tensor.matmul_mx(
+                        out=bank[:, starts[g] - lo : starts[g] - lo + cols],
+                        lhsT=w2w[e // 2][:, e % 2, 2 * j * P : 2 * (j + 1) * P].bitcast(FP4X4),
+                        lhsT_scale=w2p[:, e, :].bitcast(U8)[:, j * P : (j + 1) * P],
+                        rhs=h[g][0][:].bitcast(FP8X4), rhs_scale=h[g][1][:], start=True, stop=True,
+                    )
+            if hi - lo == P:
+                nc.vector.tensor_copy(y_sb[j][:, lo:hi], bank[:, 0 : hi - lo])
+            else:
+                nc.scalar.copy(y_sb[j][:, lo:hi], bank[:, 0 : hi - lo])
+
+        gathered = [gather(0)]
+        for g, cols in enumerate(GROUPS):
+            e = starts[g] // C
+            if g + 1 < len(GROUPS):
+                gathered.append(gather(g + 1))
+            h.append(hidden(
+                "g%d" % g, cols, gathered[g][0][:], gathered[g][1][:],
+                w1w[e][:].bitcast(FP4X4), w1p[:, e, :].bitcast(U8), g in TURN_COPY_ON_VECTOR,
+            ))
+            for lo, hi in Y0_BANKS:
+                if hi == starts[g] + cols:
+                    second(0, lo, hi)
+
+        hs = []
+        for half in range(2):
+            cols = slice(half * 256, (half + 1) * 256)
+            hs.append(hidden(
+                "s%d" % half, 256, xw[:, cols], xs[:].bitcast(U8)[:, cols],
+                w1sw[:].bitcast(FP8X4), w1sp[:].bitcast(U8), False,
+            ))
+
+        def routed_second(j):
+            for lo in range(0, SLOTS, 512):
+                second(j, lo, lo + 512)
+
+        def shared_second(j):
+            bank = next_bank("sum", sum_banks)
+            for half in range(2):
+                nc.tensor.matmul_mx(
+                    out=bank[:, half * 256 : (half + 1) * 256],
+                    lhsT=w2sw[:, j * P : (j + 1) * P].bitcast(FP8X4),
+                    lhsT_scale=w2sp[:].bitcast(U8)[:, j * P : (j + 1) * P],
+                    rhs=hs[half][0][:].bitcast(FP8X4), rhs_scale=hs[half][1][:], start=True, stop=True,
+                )
+            ys = held([P, T], F32, "ys%d" % j)
+            nc.scalar.copy(ys[:], bank[:])
+            return ys
+
+        def fetch(j, r):
+            term = held([P, T], F32, "term%d_%d" % (j, r))
+            nc.vector.tensor_tensor(term[:], y_sb[j][:].indirect(pos_sb[r][:]), gate_sb[r][:], MULT)
+            return term
+
+        def add_up(j, terms):
+            bank = next_bank("sum", sum_banks)
+            blocks = T // P
+            for i, term in enumerate(terms):
+                for b in range(blocks):
+                    nc.tensor.matmul(
+                        bank[:, b * P : (b + 1) * P], lhsT=term[:, b * P : (b + 1) * P], rhs=ident[:],
+                        start=(i == 0 and b == 0), stop=(i == len(terms) - 1 and b == blocks - 1),
+                        is_transpose=True,
+                    )
+            flipped = held([P, T], F32, "flipped%d" % j)
+            nc.scalar.copy(flipped[:], bank[:])
+            back = next_bank("sum", sum_banks)
+            for b in range(blocks):
+                nc.tensor.transpose(back[:, b * P : (b + 1) * P], flipped[:, b * P : (b + 1) * P], ident[:])
+            return back
+
+        def finish(j, back, last):
+            res = held([P, T], F32, "res%d" % j)
+            if last is None:
+                nc.scalar.copy(res[:], back[:])
+            else:
+                nc.vector.tensor_tensor(res[:], back[:], last[:], ADD)
+            nc.sync.dma_start(out[j * P : (j + 1) * P, :], res[:])
+
+        routed_second(1)
+        terms0 = [fetch(0, r) for r in range(TOP)]
+        routed_second(2)
+        ys0 = shared_second(0)
+        terms1 = [fetch(1, r) for r in range(TOP)]
+        routed_second(3)
+        finish(0, add_up(0, [ys0] + terms0), None)
+        ys1, ys2, ys3 = shared_second(1), shared_second(2), shared_second(3)
+        terms2 = [fetch(2, r) for r in range(TOP - 1)]
+        finish(1, add_up(1, [ys1] + terms1), None)
+        terms3 = [fetch(3, r) for r in range(TOP - 1)]
+        back2 = add_up(2, [ys2] + terms2)
+        back3 = add_up(3, [ys3] + terms3)
+        last2 = fetch(2, TOP - 1)
+        half = T // 2
+        last3 = [held([P, half], F32, "last3_%d" % i) for i in range(2)]
+        res3 = [held([P, half], F32, "res3_%d" % i) for i in range(2)]
+        for i in range(2):
+            picks = pos_sb[TOP - 1][:, i * half // 16 : (i + 1) * half // 16]
+            cols = slice(i * half, (i + 1) * half)
+            nc.vector.tensor_tensor(last3[i][:], y_sb[3][:].indirect(picks), gate_sb[TOP - 1][:, cols], MULT)
+            if i == 0:
+                finish(2, back2, last2)
+        for i in range(2):
+            cols = slice(i * half, (i + 1) * half)
+            nc.vector.tensor_tensor(res3[i][:], back3[:, cols], last3[i][:], ADD)
+            nc.sync.dma_start(out[3 * P : 4 * P, cols], res3[i][:])

@@ -20,9 +20,20 @@ SILU = mybir.ActivationFunctionType.Silu
 MULT = mybir.AluOpType.mult
 ADD = mybir.AluOpType.add
 
-GROUPS = [128, 128, 256, 256, 256, 256, 128, 128]
-TURN_COPY_ON_VECTOR = (3, 5, 6, 7)
-Y0_BANKS = [(0, 512), (512, 1024), (1024, 1408), (1408, 1536)]
+GROUPS = [256, 256, 256, 256, 256, 256]
+TURN_COPY_ON_VECTOR = (1, 2, 3, 6, 7)
+SHARED_COPY_ON_VECTOR = ()
+WORD_RING = 3
+BYTE_RING = 4
+AHEAD = 2
+Y_COPY_ON_VECTOR = ((0, 1024), (0, 1408))
+LOADS = [('s', 'xs'), ('a', 'w1p'), ('s', ('w1', 1, 3)), ('s', ('w1', 0, 1)), ('s', 'w2sp'), ('s', 'w1sw'), ('s', ('gate', 2)), ('s', ('pos', 1)), ('s', ('w1', 3, 6)), ('s', ('pos', 0)), ('a', 'xw'), ('s', ('gate', 1)), ('a', ('pos', 2)), ('s', ('w2', 2, 6)), ('a', ('w2', 0, 2)), ('s', ('gate', 0)), ('s', 'w2p'), ('s', 'w2sw'), ('s', 'w1sp')]
+LAST_ON_VECTOR = (2, 3)
+YS_BANKS = (6, 7, 0, 4)
+S_BANKS = (3, 5, 5, 1)
+B_BANKS = (6, 2, 2, 6)
+STEPS = [('y', 1, 0), ('y', 1, 1), ('h', 0), ('y', 1, 2), ('h', 1), ('y', 3, 1), ('y', 3, 0), ('y', 2, 2), ('y', 3, 2), ('G', 1, 0), ('G', 0, 0), ('G', 0, 1), ('G', 1, 2), ('G', 0, 2), ('G', 3, 0), ('y', 2, 1), ('y', 2, 0), ('S', 0), ('G', 3, 1), ('G', 2, 0), ('ys', 0), ('ys', 2), ('G', 1, 1), ('ys', 1), ('ys', 3), ('S', 1), ('G', 2, 1), ('S', 3), ('B', 0), ('L', 3, 1), ('B', 1), ('S', 2), ('B', 3), ('G', 2, 2), ('F', 3, 1), ('B', 2), ('W', 2), ('L', 3, 0), ('F', 3, 0)]
+Y0_BANKS = [(0, 512), (512, 1024), (1024, 1280), (1280, 1536)]
 
 
 def tile_moe_shf_mlp_silu_kernel(
@@ -44,15 +55,15 @@ def tile_moe_shf_mlp_silu_kernel(
         pos_sb = [keep.tile([P, T // 16], U16, name="pos_sb%d" % r) for r in range(TOP)]
         xw = held([P, T], I32, "xw")
         xs = held([P, T // 4], I32, "xs")
-        w1w = [held([P, 2 * H], U8, "w1w%d" % e) for e in range(E)]
-        w2w = [held([P, 2, 2 * N], U8, "w2w%d" % e) for e in range(E // 2)]
+        w1w = held([P, E, 2 * H], U8, "w1w")
+        w2w = held([P, E, 2 * N], U8, "w2w")
         w1p = held([P, E, H // 4], I32, "w1p")
         w2p = held([P, E, N // 4], I32, "w2p")
         w1sw = held([P, H], I32, "w1sw")
         w2sw = held([P, N], I32, "w2sw")
         w1sp = held([P, H // 4], I32, "w1sp")
         w2sp = held([P, N // 4], I32, "w2sp")
-        gate_sb = [held([P, T], F32, "gate_sb%d" % r) for r in range(TOP)]
+        gate_sb = held([P, TOP, T], F32, "gate_sb")
         ident = held([P, P], F32, "ident")
         warm = held([P, 8], F32, "warm")
 
@@ -62,8 +73,12 @@ def tile_moe_shf_mlp_silu_kernel(
         nc.scalar.activation(warm[:], warm[:], SILU)
         make_identity(nc, ident[:])
 
-        def load_words(tile_ap, dram):
-            nc.sync.dma_start(tile_ap, dram[0].rearrange("p n d -> p (n d)").bitcast(I32))
+        def load_words(queue, tile_ap, dram):
+            queue.dma_start(tile_ap, dram[0].rearrange("p n d -> p (n d)").bitcast(I32))
+
+        def load_experts(queue, tile, dram, lo, hi):
+            rows = dram[lo:hi, 0].rearrange("e p n -> p e n")
+            queue.dma_start(tile[:, lo:hi, :].bitcast(I32), rows.bitcast(I32))
 
         def load_plane(queue, plane, dram):
             for q in range(4):
@@ -75,42 +90,51 @@ def tile_moe_shf_mlp_silu_kernel(
                 queue.dma_start(plane[32 * q : 32 * q + 4, :, :], rows.bitcast(I32))
 
         nc.sync.dma_start(offs_sb[:], offs)
-        for q in range(4):
-            rows = x_scales[0, 4 * q : 4 * q + 4, :].bitcast(I32)
-            nc.sync.dma_start(xs[32 * q : 32 * q + 32, :], rows.unsqueeze(0).to_broadcast([8, 4, T // 4]))
-        load_words(xw[:], x_words)
-        nc.sync.dma_start(w1w[0][:].bitcast(I32), w1_words[0, 0].bitcast(I32))
-        load_planes(nc.sync, w1p, w1_scales)
-        for e in range(1, E):
-            nc.sync.dma_start(w1w[e][:].bitcast(I32), w1_words[e, 0].bitcast(I32))
-        load_planes(nc.sync, w2p, w2_scales)
-        for e in range(E // 2):
-            pair = w2_words[2 * e : 2 * e + 2, 0].rearrange("e p n -> p e n")
-            nc.sync.dma_start(w2w[e][:].bitcast(I32), pair.bitcast(I32))
-        load_words(w1sw[:], w1s_words)
-        load_plane(nc.sync, w1sp, w1s_scales)
-        for r, pos in enumerate((pos1, pos2, pos3)):
-            nc.sync.dma_start(pos_sb[r][:], pos)
-            nc.sync.dma_start(gate_sb[r][:], gate[r])
-        load_words(w2sw[:], w2s_words)
-        load_plane(nc.sync, w2sp, w2s_scales)
+        queues = {"s": nc.sync, "a": nc.scalar}
+        for qn, what in LOADS:
+            queue = queues[qn]
+            if what == "xs":
+                for q in range(4):
+                    rows = x_scales[0, 4 * q : 4 * q + 4, :].bitcast(I32)
+                    queue.dma_start(xs[32 * q : 32 * q + 32, :], rows.unsqueeze(0).to_broadcast([8, 4, T // 4]))
+            elif what == "xw":
+                load_words(queue, xw[:], x_words)
+            elif what[0] == "w1":
+                load_experts(queue, w1w, w1_words, what[1], what[2])
+            elif what[0] == "w2":
+                load_experts(queue, w2w, w2_words, what[1], what[2])
+            elif what == "w1p":
+                load_planes(queue, w1p, w1_scales)
+            elif what == "w2p":
+                load_planes(queue, w2p, w2_scales)
+            elif what == "w1sw":
+                load_words(queue, w1sw[:], w1s_words)
+            elif what == "w2sw":
+                load_words(queue, w2sw[:], w2s_words)
+            elif what == "w1sp":
+                load_plane(queue, w1sp, w1s_scales)
+            elif what == "w2sp":
+                load_plane(queue, w2sp, w2s_scales)
+            elif what[0] == "pos":
+                nc.sync.dma_start(pos_sb[what[1]][:], (pos1, pos2, pos3)[what[1]])
+            elif what[0] == "gate":
+                queue.dma_start(gate_sb[:, what[1], :], gate[what[1]])
 
         first_banks = banks[0:3]
         turn_banks = banks[3:5]
         y_banks = banks[5:8]
-        sum_banks = banks[0:5]
-        used = {"first": 0, "turn": 0, "y": 0, "sum": 0}
+        used = {"first": 0, "turn": 0, "y": 0}
 
         def next_bank(role, ring):
             bank = ring[used[role] % len(ring)]
             used[role] = used[role] + 1
             return bank
 
-        def hidden(name, cols, x_codes, x_plane, w_codes, w_plane, copy_on_vector):
+        def hidden(name, cols, x_codes, x_plane, w_codes, w_plane, copy_on_vector, first_ring):
             tiles = cols // P
             turned = next_bank("turn", turn_banks)
             for a in range(tiles):
-                acc = next_bank("first", first_banks)
+                acc = next_bank("first", first_ring)
                 nc.tensor.matmul_mx(
                     out=acc[:], lhsT=x_codes[:, a * P : (a + 1) * P].bitcast(FP8X4),
                     lhsT_scale=x_plane[:, a * P : (a + 1) * P], rhs=w_codes, rhs_scale=w_plane,
@@ -143,8 +167,8 @@ def tile_moe_shf_mlp_silu_kernel(
         def gather(g):
             cols = GROUPS[g]
             picks = offs_sb[:, starts[g] // 16 : (starts[g] + cols) // 16]
-            xg = ring.tile([P, cols], U32, name="xg", bufs=3, align_bytes=64)
-            xgp = ring.tile([P, cols], U8, name="xgp", bufs=2, align_bytes=64)
+            xg = ring.tile([P, cols], U32, name="xg", bufs=WORD_RING, align_bytes=64)
+            xgp = ring.tile([P, cols], U8, name="xgp", bufs=BYTE_RING, align_bytes=64)
             nc.vector.tensor_copy(xgp[:], xs[:].bitcast(U8).indirect(picks))
             nc.vector.tensor_copy(xg[:], xw[:].bitcast(U32).indirect(picks))
             return xg, xgp
@@ -158,74 +182,67 @@ def tile_moe_shf_mlp_silu_kernel(
                     e = starts[g] // C
                     nc.tensor.matmul_mx(
                         out=bank[:, starts[g] - lo : starts[g] - lo + cols],
-                        lhsT=w2w[e // 2][:, e % 2, 2 * j * P : 2 * (j + 1) * P].bitcast(FP4X4),
+                        lhsT=w2w[:, e, 2 * j * P : 2 * (j + 1) * P].bitcast(FP4X4),
                         lhsT_scale=w2p[:, e, :].bitcast(U8)[:, j * P : (j + 1) * P],
                         rhs=h[g][0][:].bitcast(FP8X4), rhs_scale=h[g][1][:], start=True, stop=True,
                     )
-            if hi - lo == P:
+            if (j, lo) in Y_COPY_ON_VECTOR:
                 nc.vector.tensor_copy(y_sb[j][:, lo:hi], bank[:, 0 : hi - lo])
             else:
                 nc.scalar.copy(y_sb[j][:, lo:hi], bank[:, 0 : hi - lo])
 
-        gathered = [gather(0)]
+        gathered = [gather(g) for g in range(AHEAD)]
         for g, cols in enumerate(GROUPS):
             e = starts[g] // C
-            if g + 1 < len(GROUPS):
-                gathered.append(gather(g + 1))
+            if g + AHEAD < len(GROUPS):
+                gathered.append(gather(g + AHEAD))
             h.append(hidden(
                 "g%d" % g, cols, gathered[g][0][:], gathered[g][1][:],
-                w1w[e][:].bitcast(FP4X4), w1p[:, e, :].bitcast(U8), g in TURN_COPY_ON_VECTOR,
+                w1w[:, e, :].bitcast(FP4X4), w1p[:, e, :].bitcast(U8), g in TURN_COPY_ON_VECTOR, first_banks,
             ))
             for lo, hi in Y0_BANKS:
                 if hi == starts[g] + cols:
                     second(0, lo, hi)
 
-        hs = []
-        for half in range(2):
-            cols = slice(half * 256, (half + 1) * 256)
-            hs.append(hidden(
-                "s%d" % half, 256, xw[:, cols], xs[:].bitcast(U8)[:, cols],
-                w1sw[:].bitcast(FP8X4), w1sp[:].bitcast(U8), False,
-            ))
-
-        def routed_second(j):
-            for lo in range(0, SLOTS, 512):
-                second(j, lo, lo + 512)
-
-        def shared_second(j):
-            bank = next_bank("sum", sum_banks)
-            for half in range(2):
-                nc.tensor.matmul_mx(
-                    out=bank[:, half * 256 : (half + 1) * 256],
-                    lhsT=w2sw[:, j * P : (j + 1) * P].bitcast(FP8X4),
-                    lhsT_scale=w2sp[:].bitcast(U8)[:, j * P : (j + 1) * P],
-                    rhs=hs[half][0][:].bitcast(FP8X4), rhs_scale=hs[half][1][:], start=True, stop=True,
-                )
-            ys = held([P, T], F32, "ys%d" % j)
+        def shared_second(b, bank):
+            codes, plane = hs[b // 2]
+            cols = slice((b % 2) * P, (b % 2 + 1) * P)
+            nc.tensor.matmul_mx(
+                out=bank[:], lhsT=codes[:, cols].bitcast(FP8X4), lhsT_scale=plane[:, cols],
+                rhs=w2sw[:].bitcast(FP8X4), rhs_scale=w2sp[:].bitcast(U8), start=True, stop=True,
+            )
+            ys = held([P, N], F32, "ys%d" % b)
             nc.scalar.copy(ys[:], bank[:])
             return ys
 
         def fetch(j, r):
             term = held([P, T], F32, "term%d_%d" % (j, r))
-            nc.vector.tensor_tensor(term[:], y_sb[j][:].indirect(pos_sb[r][:]), gate_sb[r][:], MULT)
+            nc.vector.tensor_tensor(term[:], y_sb[j][:].indirect(pos_sb[r][:]), gate_sb[:, r, :], MULT)
             return term
 
-        def add_up(j, terms):
-            bank = next_bank("sum", sum_banks)
-            blocks = T // P
-            for i, term in enumerate(terms):
+        blocks = T // P
+
+        def turn_add(bank, sources):
+            for i, source in enumerate(sources):
                 for b in range(blocks):
                     nc.tensor.matmul(
-                        bank[:, b * P : (b + 1) * P], lhsT=term[:, b * P : (b + 1) * P], rhs=ident[:],
-                        start=(i == 0 and b == 0), stop=(i == len(terms) - 1 and b == blocks - 1),
+                        bank[:, b * P : (b + 1) * P], lhsT=source[b], rhs=ident[:],
+                        start=(i == 0 and b == 0), stop=(i == len(sources) - 1 and b == blocks - 1),
                         is_transpose=True,
                     )
+
+        def cut(tile):
+            return [tile[:, b * P : (b + 1) * P] for b in range(blocks)]
+
+        def add_terms(j, terms, bank):
+            turn_add(bank, [cut(term) for term in terms])
             flipped = held([P, T], F32, "flipped%d" % j)
             nc.scalar.copy(flipped[:], bank[:])
-            back = next_bank("sum", sum_banks)
-            for b in range(blocks):
-                nc.tensor.transpose(back[:, b * P : (b + 1) * P], flipped[:, b * P : (b + 1) * P], ident[:])
-            return back
+            return flipped
+
+        def turn_back(j, flipped, bank):
+            turn_add(bank, [[ys_t[b][:, j * P : (j + 1) * P] for b in range(blocks)], cut(flipped)])
+            return bank
 
         def finish(j, back, last):
             res = held([P, T], F32, "res%d" % j)
@@ -235,30 +252,44 @@ def tile_moe_shf_mlp_silu_kernel(
                 nc.vector.tensor_tensor(res[:], back[:], last[:], ADD)
             nc.sync.dma_start(out[j * P : (j + 1) * P, :], res[:])
 
-        routed_second(1)
-        terms0 = [fetch(0, r) for r in range(TOP)]
-        routed_second(2)
-        ys0 = shared_second(0)
-        terms1 = [fetch(1, r) for r in range(TOP)]
-        routed_second(3)
-        finish(0, add_up(0, [ys0] + terms0), None)
-        ys1, ys2, ys3 = shared_second(1), shared_second(2), shared_second(3)
-        terms2 = [fetch(2, r) for r in range(TOP - 1)]
-        finish(1, add_up(1, [ys1] + terms1), None)
-        terms3 = [fetch(3, r) for r in range(TOP - 1)]
-        back2 = add_up(2, [ys2] + terms2)
-        back3 = add_up(3, [ys3] + terms3)
-        last2 = fetch(2, TOP - 1)
         half = T // 2
-        last3 = [held([P, half], F32, "last3_%d" % i) for i in range(2)]
-        res3 = [held([P, half], F32, "res3_%d" % i) for i in range(2)]
-        for i in range(2):
+        hs, ys_t, terms, flips, backs = {}, {}, {}, {}, {}
+
+        def last_half(j, i):
             picks = pos_sb[TOP - 1][:, i * half // 16 : (i + 1) * half // 16]
-            cols = slice(i * half, (i + 1) * half)
-            nc.vector.tensor_tensor(last3[i][:], y_sb[3][:].indirect(picks), gate_sb[TOP - 1][:, cols], MULT)
-            if i == 0:
-                finish(2, back2, last2)
-        for i in range(2):
-            cols = slice(i * half, (i + 1) * half)
-            nc.vector.tensor_tensor(res3[i][:], back3[:, cols], last3[i][:], ADD)
-            nc.sync.dma_start(out[3 * P : 4 * P, cols], res3[i][:])
+            term = held([P, half], F32, "last%d_%d" % (j, i))
+            nc.vector.tensor_tensor(term[:], y_sb[j][:].indirect(picks), gate_sb[:, TOP - 1, i * half : (i + 1) * half], MULT)
+            return term
+
+        for step in STEPS:
+            kind = step[0]
+            if kind == "y":
+                second(step[1], step[2] * 512, (step[2] + 1) * 512)
+            elif kind == "h":
+                cols = slice(step[1] * 256, (step[1] + 1) * 256)
+                hs[step[1]] = hidden(
+                    "s%d" % step[1], 256, xw[:, cols], xs[:].bitcast(U8)[:, cols],
+                    w1sw[:].bitcast(FP8X4), w1sp[:].bitcast(U8), step[1] in SHARED_COPY_ON_VECTOR, banks[0:2],
+                )
+            elif kind == "ys":
+                ys_t[step[1]] = shared_second(step[1], banks[YS_BANKS[step[1]]])
+            elif kind == "G":
+                terms[step[1], step[2]] = fetch(step[1], step[2])
+            elif kind == "L":
+                terms[step[1], "L", step[2]] = last_half(step[1], step[2])
+            elif kind == "S":
+                j = step[1]
+                flips[j] = add_terms(j, [terms[j, r] for r in range(TOP if j not in LAST_ON_VECTOR else TOP - 1)], banks[S_BANKS[j]])
+            elif kind == "B":
+                j = step[1]
+                backs[j] = turn_back(j, flips[j], banks[B_BANKS[j]])
+                if j not in LAST_ON_VECTOR:
+                    finish(j, backs[j], None)
+            elif kind == "F":
+                j, i = step[1], step[2]
+                cols = slice(i * half, (i + 1) * half)
+                res = held([P, half], F32, "res%d_%d" % (j, i))
+                nc.vector.tensor_tensor(res[:], backs[j][:, cols], terms[j, "L", i][:], ADD)
+                nc.sync.dma_start(out[j * P : (j + 1) * P, cols], res[:])
+            elif kind == "W":
+                finish(step[1], backs[step[1]], terms[step[1], TOP - 1])

@@ -21,18 +21,27 @@ MULT = mybir.AluOpType.mult
 ADD = mybir.AluOpType.add
 
 GROUPS = [256, 256, 256, 256, 256, 256]
-TURN_COPY_ON_VECTOR = (1, 2, 3, 6, 7)
+TURN_COPY_ON_VECTOR = (2, 3, 6)
 SHARED_COPY_ON_VECTOR = ()
 WORD_RING = 3
-BYTE_RING = 4
-AHEAD = 2
-Y_COPY_ON_VECTOR = ((0, 1024), (0, 1408))
-LOADS = [('s', 'xs'), ('a', 'w1p'), ('s', ('w1', 1, 3)), ('s', ('w1', 0, 1)), ('s', 'w2sp'), ('s', 'w1sw'), ('s', ('gate', 2)), ('s', ('pos', 1)), ('s', ('w1', 3, 6)), ('s', ('pos', 0)), ('a', 'xw'), ('s', ('gate', 1)), ('a', ('pos', 2)), ('s', ('w2', 2, 6)), ('a', ('w2', 0, 2)), ('s', ('gate', 0)), ('s', 'w2p'), ('s', 'w2sw'), ('s', 'w1sp')]
+DIRECT = (3, 4, 5)
+PERMUTE_AHEAD = 0
+W1P_CUT = 6
+MEMSETS = ['w1pb', 'w1sp', 'w2p', 'w2sp', 'w1pa']
+W1_CUTS = (0, 1, 4, 6)
+W2_CUTS = (0, 4, 6)
+WORD_FIRST = False
+SHARED_AT = (7, 6)
+YS_ON_VECTOR = ()
+BYTE_RING = 3
+AHEAD = 1
+Y_COPY_ON_VECTOR = ((0, 512), (0, 1280), (0, 1408))
+LOADS = [('s', 'xs'), ('s', 'xw'), ('s', ('w2', 1)), ('s', ('w1', 0)), ('s', 'w1pa'), ('s', ('gate', 1)), ('s', 'w1pb'), ('s', ('w1', 1)), ('s', ('w1', 2)), ('s', 'w1sp'), ('s', ('pos', 2)), ('a', ('pos', 1)), ('s', ('gate', 0)), ('s', 'w2sp'), ('s', ('w2', 0)), ('s', ('pos', 0)), ('s', ('gate', 2)), ('s', 'w2p'), ('s', 'w1sw'), ('s', 'w2sw')]
 LAST_ON_VECTOR = (2, 3)
-YS_BANKS = (6, 7, 0, 4)
-S_BANKS = (3, 5, 5, 1)
-B_BANKS = (6, 2, 2, 6)
-STEPS = [('y', 1, 0), ('y', 1, 1), ('h', 0), ('y', 1, 2), ('h', 1), ('y', 3, 1), ('y', 3, 0), ('y', 2, 2), ('y', 3, 2), ('G', 1, 0), ('G', 0, 0), ('G', 0, 1), ('G', 1, 2), ('G', 0, 2), ('G', 3, 0), ('y', 2, 1), ('y', 2, 0), ('S', 0), ('G', 3, 1), ('G', 2, 0), ('ys', 0), ('ys', 2), ('G', 1, 1), ('ys', 1), ('ys', 3), ('S', 1), ('G', 2, 1), ('S', 3), ('B', 0), ('L', 3, 1), ('B', 1), ('S', 2), ('B', 3), ('G', 2, 2), ('F', 3, 1), ('B', 2), ('W', 2), ('L', 3, 0), ('F', 3, 0)]
+YS_BANKS = (6, 4, 5, 2)
+S_BANKS = (1, 0, 2, 3)
+B_BANKS = (4, 1, 5, 3)
+STEPS = [('h', 0), ('y', 2, 2), ('G', 0, 0), ('y', 1, 1), ('y', 1, 0), ('y', 1, 2), ('h', 1), ('y', 3, 1), ('G', 1, 2), ('y', 3, 2), ('y', 2, 0), ('G', 1, 0), ('y', 3, 0), ('y', 2, 1), ('G', 0, 2), ('G', 0, 1), ('ys', 1), ('G', 1, 1), ('G', 3, 0), ('S', 0), ('G', 3, 1), ('ys', 2), ('ys', 0), ('ys', 3), ('G', 2, 0), ('S', 1), ('S', 3), ('B', 0), ('B', 1), ('G', 2, 1), ('S', 2), ('L', 3, 1), ('G', 2, 2), ('B', 3), ('F', 3, 1), ('B', 2), ('W', 2), ('L', 3, 0), ('F', 3, 0)]
 Y0_BANKS = [(0, 512), (512, 1024), (1024, 1280), (1280, 1536)]
 
 
@@ -67,8 +76,10 @@ def tile_moe_shf_mlp_silu_kernel(
         ident = held([P, P], F32, "ident")
         warm = held([P, 8], F32, "warm")
 
-        for plane in (w1p, w2p, w1sp, w2sp):
-            nc.vector.memset(plane[:], 0)
+        planes = {"w2p": w2p[:], "w1sp": w1sp[:], "w2sp": w2sp[:], "w1pa": w1p[:, 0:W1P_CUT, :], "w1pb": w1p[:, W1P_CUT:E, :]}
+        for name in MEMSETS:
+            if name != "w1pb" or W1P_CUT < E:
+                nc.vector.memset(planes[name], 0)
         nc.gpsimd.memset(warm[:], 0.0)
         nc.scalar.activation(warm[:], warm[:], SILU)
         make_identity(nc, ident[:])
@@ -100,13 +111,16 @@ def tile_moe_shf_mlp_silu_kernel(
             elif what == "xw":
                 load_words(queue, xw[:], x_words)
             elif what[0] == "w1":
-                load_experts(queue, w1w, w1_words, what[1], what[2])
+                load_experts(queue, w1w, w1_words, W1_CUTS[what[1]], W1_CUTS[what[1] + 1])
             elif what[0] == "w2":
-                load_experts(queue, w2w, w2_words, what[1], what[2])
-            elif what == "w1p":
-                load_planes(queue, w1p, w1_scales)
+                load_experts(queue, w2w, w2_words, W2_CUTS[what[1]], W2_CUTS[what[1] + 1])
+            elif what == "w1pa":
+                load_planes(queue, w1p[:, 0:W1P_CUT, :], w1_scales[0:W1P_CUT])
+            elif what == "w1pb":
+                if W1P_CUT < E:
+                    load_planes(queue, w1p[:, W1P_CUT:E, :], w1_scales[W1P_CUT:E])
             elif what == "w2p":
-                load_planes(queue, w2p, w2_scales)
+                load_planes(queue, w2p[:], w2_scales)
             elif what == "w1sw":
                 load_words(queue, w1sw[:], w1s_words)
             elif what == "w2sw":
@@ -161,6 +175,35 @@ def tile_moe_shf_mlp_silu_kernel(
             nc.vector.quantize_mx(out=codes[:].bitcast(FP8X4), scales=plane[:], in_=grouped[:].bitcast(BF16))
             return codes, plane
 
+        def permuted(e):
+            words = held([P, H], U16, "w1_words_by_t%d" % e)
+            plane = held([P, H], U8, "w1_plane_by_t%d" % e)
+            for dst, src in ((words, w1w[:, e, :].bitcast(U16)), (plane, w1p[:, e, :].bitcast(U8))):
+                nc.vector.tensor_copy(
+                    dst[:].rearrange("p (t m) -> p t m", t=4), src.rearrange("p (m t) -> p t m", t=4)
+                )
+            return words, plane
+
+        def hidden_direct(name, cols, x_codes, x_plane, words, plane):
+            grouped = held([P, 4 * cols], BF16, "grouped_" + name)
+            for a in range(cols // P):
+                acc = next_bank("first", first_banks)
+                slots = slice(a * P, (a + 1) * P)
+                for t in range(4):
+                    nc.tensor.matmul_mx(
+                        out=acc[:, t * P : (t + 1) * P], lhsT=words[:, t * P : (t + 1) * P].bitcast(FP4X4),
+                        lhsT_scale=plane[:, t * P : (t + 1) * P], rhs=x_codes[:, slots].bitcast(FP8X4),
+                        rhs_scale=x_plane[:, slots], start=True, stop=True,
+                    )
+                nc.scalar.activation(
+                    grouped[:, a * H : (a + 1) * H].rearrange("p (s t) -> p s t", t=4),
+                    acc[:].rearrange("p (t s) -> p s t", t=4), SILU,
+                )
+            codes = held([P, cols], U32, "codes_" + name)
+            scales = held([P, cols], U8, "plane_" + name)
+            nc.vector.quantize_mx(out=codes[:].bitcast(FP8X4), scales=scales[:], in_=grouped[:])
+            return codes, scales
+
         y_sb = [held([P, SLOTS], F32, "y_sb%d" % j) for j in range(N // P)]
         starts = [sum(GROUPS[:g]) for g in range(len(GROUPS))]
 
@@ -169,8 +212,11 @@ def tile_moe_shf_mlp_silu_kernel(
             picks = offs_sb[:, starts[g] // 16 : (starts[g] + cols) // 16]
             xg = ring.tile([P, cols], U32, name="xg", bufs=WORD_RING, align_bytes=64)
             xgp = ring.tile([P, cols], U8, name="xgp", bufs=BYTE_RING, align_bytes=64)
+            if WORD_FIRST:
+                nc.vector.tensor_copy(xg[:], xw[:].bitcast(U32).indirect(picks))
             nc.vector.tensor_copy(xgp[:], xs[:].bitcast(U8).indirect(picks))
-            nc.vector.tensor_copy(xg[:], xw[:].bitcast(U32).indirect(picks))
+            if not WORD_FIRST:
+                nc.vector.tensor_copy(xg[:], xw[:].bitcast(U32).indirect(picks))
             return xg, xgp
 
         h = []
@@ -191,15 +237,33 @@ def tile_moe_shf_mlp_silu_kernel(
             else:
                 nc.scalar.copy(y_sb[j][:, lo:hi], bank[:, 0 : hi - lo])
 
+        hs, by_t = {}, {}
+
+        def shared_first(i, ring_banks):
+            cols = slice(i * 256, (i + 1) * 256)
+            hs[i] = hidden(
+                "s%d" % i, 256, xw[:, cols], xs[:].bitcast(U8)[:, cols],
+                w1sw[:].bitcast(FP8X4), w1sp[:].bitcast(U8), i in SHARED_COPY_ON_VECTOR, ring_banks,
+            )
+
         gathered = [gather(g) for g in range(AHEAD)]
         for g, cols in enumerate(GROUPS):
             e = starts[g] // C
+            for i in range(2):
+                if SHARED_AT[i] == g:
+                    shared_first(i, first_banks)
             if g + AHEAD < len(GROUPS):
                 gathered.append(gather(g + AHEAD))
-            h.append(hidden(
-                "g%d" % g, cols, gathered[g][0][:], gathered[g][1][:],
-                w1w[:, e, :].bitcast(FP4X4), w1p[:, e, :].bitcast(U8), g in TURN_COPY_ON_VECTOR, first_banks,
-            ))
+            for later in DIRECT:
+                if max(later - PERMUTE_AHEAD, 0) == e and later not in by_t:
+                    by_t[later] = permuted(later)
+            if e in DIRECT:
+                h.append(hidden_direct("g%d" % g, cols, gathered[g][0][:], gathered[g][1][:], *by_t[e]))
+            else:
+                h.append(hidden(
+                    "g%d" % g, cols, gathered[g][0][:], gathered[g][1][:],
+                    w1w[:, e, :].bitcast(FP4X4), w1p[:, e, :].bitcast(U8), g in TURN_COPY_ON_VECTOR, first_banks,
+                ))
             for lo, hi in Y0_BANKS:
                 if hi == starts[g] + cols:
                     second(0, lo, hi)
@@ -212,7 +276,10 @@ def tile_moe_shf_mlp_silu_kernel(
                 rhs=w2sw[:].bitcast(FP8X4), rhs_scale=w2sp[:].bitcast(U8), start=True, stop=True,
             )
             ys = held([P, N], F32, "ys%d" % b)
-            nc.scalar.copy(ys[:], bank[:])
+            if b in YS_ON_VECTOR:
+                nc.vector.tensor_copy(ys[:], bank[:])
+            else:
+                nc.scalar.copy(ys[:], bank[:])
             return ys
 
         def fetch(j, r):
@@ -253,7 +320,7 @@ def tile_moe_shf_mlp_silu_kernel(
             nc.sync.dma_start(out[j * P : (j + 1) * P, :], res[:])
 
         half = T // 2
-        hs, ys_t, terms, flips, backs = {}, {}, {}, {}, {}
+        ys_t, terms, flips, backs = {}, {}, {}, {}
 
         def last_half(j, i):
             picks = pos_sb[TOP - 1][:, i * half // 16 : (i + 1) * half // 16]
@@ -266,11 +333,8 @@ def tile_moe_shf_mlp_silu_kernel(
             if kind == "y":
                 second(step[1], step[2] * 512, (step[2] + 1) * 512)
             elif kind == "h":
-                cols = slice(step[1] * 256, (step[1] + 1) * 256)
-                hs[step[1]] = hidden(
-                    "s%d" % step[1], 256, xw[:, cols], xs[:].bitcast(U8)[:, cols],
-                    w1sw[:].bitcast(FP8X4), w1sp[:].bitcast(U8), step[1] in SHARED_COPY_ON_VECTOR, banks[0:2],
-                )
+                if SHARED_AT[step[1]] >= len(GROUPS):
+                    shared_first(step[1], banks[0:2])
             elif kind == "ys":
                 ys_t[step[1]] = shared_second(step[1], banks[YS_BANKS[step[1]]])
             elif kind == "G":
@@ -292,4 +356,5 @@ def tile_moe_shf_mlp_silu_kernel(
                 nc.vector.tensor_tensor(res[:], backs[j][:, cols], terms[j, "L", i][:], ADD)
                 nc.sync.dma_start(out[j * P : (j + 1) * P, cols], res[:])
             elif kind == "W":
-                finish(step[1], backs[step[1]], terms[step[1], TOP - 1])
+                if step[1] in LAST_ON_VECTOR:
+                    finish(step[1], backs[step[1]], terms[step[1], TOP - 1])

@@ -20,29 +20,32 @@ SILU = mybir.ActivationFunctionType.Silu
 MULT = mybir.AluOpType.mult
 ADD = mybir.AluOpType.add
 
-GROUPS = [256, 256, 256, 256, 256, 256]
-TURN_COPY_ON_VECTOR = (2, 3, 6)
-SHARED_COPY_ON_VECTOR = ()
+GROUPS = [256, 256, 256, 256, 256, 128, 128]
+TURN_COPY_ON_VECTOR = (2, 4)
+SHARED_COPY_ON_VECTOR = (1,)
 WORD_RING = 3
+WORDS_ON_GPSIMD = (1, 2, 5)
+PLANES_ON_GPSIMD = (3, 5)
+SHARED_DIRECT = 2
 DIRECT = (3, 4, 5)
-PERMUTE_AHEAD = 0
+PERMUTE_AHEAD = 1
 W1P_CUT = 6
-MEMSETS = ['w1pb', 'w1sp', 'w2p', 'w2sp', 'w1pa']
-W1_CUTS = (0, 1, 4, 6)
-W2_CUTS = (0, 4, 6)
-WORD_FIRST = False
-SHARED_AT = (7, 6)
+MEMSETS = ['w2sp', 'w1pb', 'w1sp', 'w1pa', 'w2p']
+W1_CUTS = (0, 1, 2, 6)
+W2_CUTS = (0, 3, 6)
+WORD_FIRST = True
+SHARED_AT = (7, 7)
 YS_ON_VECTOR = ()
 BYTE_RING = 3
 AHEAD = 1
-Y_COPY_ON_VECTOR = ((0, 512), (0, 1280), (0, 1408))
-LOADS = [('s', 'xs'), ('s', 'xw'), ('s', ('w2', 1)), ('s', ('w1', 0)), ('s', 'w1pa'), ('s', ('gate', 1)), ('s', 'w1pb'), ('s', ('w1', 1)), ('s', ('w1', 2)), ('s', 'w1sp'), ('s', ('pos', 2)), ('a', ('pos', 1)), ('s', ('gate', 0)), ('s', 'w2sp'), ('s', ('w2', 0)), ('s', ('pos', 0)), ('s', ('gate', 2)), ('s', 'w2p'), ('s', 'w1sw'), ('s', 'w2sw')]
+Y_COPY_ON_VECTOR = ((0, 512),)
+LOADS = [('s', 'xs'), ('s', ('w1', 0)), ('s', 'w1pa'), ('s', ('w1', 1)), ('s', ('w1', 2)), ('s', ('gate', 1)), ('s', ('w2', 1)), ('s', 'w1sp'), ('a', 'xw'), ('s', 'w2sw'), ('s', ('w2', 0)), ('a', ('pos', 2)), ('s', 'w2p'), ('a', ('gate', 0)), ('s', 'w1sw'), ('s', ('gate', 2)), ('a', ('pos', 0)), ('s', 'w2sp'), ('a', 'w1pb'), ('s', ('pos', 1))]
 LAST_ON_VECTOR = (2, 3)
-YS_BANKS = (6, 4, 5, 2)
-S_BANKS = (1, 0, 2, 3)
-B_BANKS = (4, 1, 5, 3)
-STEPS = [('h', 0), ('y', 2, 2), ('G', 0, 0), ('y', 1, 1), ('y', 1, 0), ('y', 1, 2), ('h', 1), ('y', 3, 1), ('G', 1, 2), ('y', 3, 2), ('y', 2, 0), ('G', 1, 0), ('y', 3, 0), ('y', 2, 1), ('G', 0, 2), ('G', 0, 1), ('ys', 1), ('G', 1, 1), ('G', 3, 0), ('S', 0), ('G', 3, 1), ('ys', 2), ('ys', 0), ('ys', 3), ('G', 2, 0), ('S', 1), ('S', 3), ('B', 0), ('B', 1), ('G', 2, 1), ('S', 2), ('L', 3, 1), ('G', 2, 2), ('B', 3), ('F', 3, 1), ('B', 2), ('W', 2), ('L', 3, 0), ('F', 3, 0)]
-Y0_BANKS = [(0, 512), (512, 1024), (1024, 1280), (1280, 1536)]
+YS_BANKS = (4, 3, 6, 5)
+S_BANKS = (0, 7, 3, 4)
+B_BANKS = (2, 0, 2, 6)
+STEPS = [('h', 0), ('G', 0, 2), ('h', 1), ('y', 1, 1), ('G', 0, 0), ('y', 1, 2), ('y', 1, 0), ('G', 1, 2), ('G', 0, 1), ('y', 2, 2), ('G', 1, 0), ('y', 3, 1), ('y', 3, 0), ('y', 2, 1), ('y', 3, 2), ('y', 2, 0), ('ys', 0), ('G', 3, 0), ('G', 3, 1), ('G', 1, 1), ('ys', 1), ('S', 0), ('G', 2, 0), ('ys', 3), ('ys', 2), ('G', 2, 1), ('S', 1), ('B', 0), ('B', 1), ('G', 2, 2), ('S', 3), ('S', 2), ('B', 3), ('B', 2), ('L', 3, 1), ('L', 3, 0), ('F', 3, 1), ('F', 3, 0), ('W', 2)]
+Y0_BANKS = [(0, 512), (512, 1024), (1024, 1408), (1408, 1536)]
 
 
 def tile_moe_shf_mlp_silu_kernel(
@@ -175,23 +178,31 @@ def tile_moe_shf_mlp_silu_kernel(
             nc.vector.quantize_mx(out=codes[:].bitcast(FP8X4), scales=plane[:], in_=grouped[:].bitcast(BF16))
             return codes, plane
 
+        def by_column(engine, dst, src):
+            engine.tensor_copy(dst.rearrange("p (t m) -> p t m", t=4), src.rearrange("p (m t) -> p t m", t=4))
+
         def permuted(e):
             words = held([P, H], U16, "w1_words_by_t%d" % e)
             plane = held([P, H], U8, "w1_plane_by_t%d" % e)
-            for dst, src in ((words, w1w[:, e, :].bitcast(U16)), (plane, w1p[:, e, :].bitcast(U8))):
-                nc.vector.tensor_copy(
-                    dst[:].rearrange("p (t m) -> p t m", t=4), src.rearrange("p (m t) -> p t m", t=4)
-                )
-            return words, plane
+            if e in WORDS_ON_GPSIMD:
+                for b in range(2):
+                    nc.gpsimd.tensor_copy(
+                        words[:].bitcast(U8).rearrange("p (t m b) -> p b t m", t=4, b=2)[:, b],
+                        w1w[:, e, :].rearrange("p (m t b) -> p b t m", t=4, b=2)[:, b],
+                    )
+            else:
+                by_column(nc.vector, words[:], w1w[:, e, :].bitcast(U16))
+            by_column(nc.gpsimd if e in PLANES_ON_GPSIMD else nc.vector, plane[:], w1p[:, e, :].bitcast(U8))
+            return words[:].bitcast(FP4X4), plane
 
-        def hidden_direct(name, cols, x_codes, x_plane, words, plane):
+        def hidden_direct(name, cols, x_codes, x_plane, words, plane, first_ring):
             grouped = held([P, 4 * cols], BF16, "grouped_" + name)
             for a in range(cols // P):
-                acc = next_bank("first", first_banks)
+                acc = next_bank("first", first_ring)
                 slots = slice(a * P, (a + 1) * P)
                 for t in range(4):
                     nc.tensor.matmul_mx(
-                        out=acc[:, t * P : (t + 1) * P], lhsT=words[:, t * P : (t + 1) * P].bitcast(FP4X4),
+                        out=acc[:, t * P : (t + 1) * P], lhsT=words[:, t * P : (t + 1) * P],
                         lhsT_scale=plane[:, t * P : (t + 1) * P], rhs=x_codes[:, slots].bitcast(FP8X4),
                         rhs_scale=x_plane[:, slots], start=True, stop=True,
                     )
@@ -241,6 +252,15 @@ def tile_moe_shf_mlp_silu_kernel(
 
         def shared_first(i, ring_banks):
             cols = slice(i * 256, (i + 1) * 256)
+            if SHARED_DIRECT:
+                if "s" not in by_t:
+                    words = held([P, H], I32, "w1s_words_by_t")
+                    plane = held([P, H], U8, "w1s_plane_by_t")
+                    by_column(nc.gpsimd if SHARED_DIRECT == 2 else nc.vector, words[:], w1sw[:])
+                    by_column(nc.gpsimd if SHARED_DIRECT == 2 else nc.vector, plane[:], w1sp[:].bitcast(U8))
+                    by_t["s"] = (words[:].bitcast(FP8X4), plane)
+                hs[i] = hidden_direct("s%d" % i, 256, xw[:, cols], xs[:].bitcast(U8)[:, cols], *by_t["s"], ring_banks)
+                return
             hs[i] = hidden(
                 "s%d" % i, 256, xw[:, cols], xs[:].bitcast(U8)[:, cols],
                 w1sw[:].bitcast(FP8X4), w1sp[:].bitcast(U8), i in SHARED_COPY_ON_VECTOR, ring_banks,
@@ -258,7 +278,7 @@ def tile_moe_shf_mlp_silu_kernel(
                 if max(later - PERMUTE_AHEAD, 0) == e and later not in by_t:
                     by_t[later] = permuted(later)
             if e in DIRECT:
-                h.append(hidden_direct("g%d" % g, cols, gathered[g][0][:], gathered[g][1][:], *by_t[e]))
+                h.append(hidden_direct("g%d" % g, cols, gathered[g][0][:], gathered[g][1][:], *by_t[e], first_banks))
             else:
                 h.append(hidden(
                     "g%d" % g, cols, gathered[g][0][:], gathered[g][1][:],

@@ -20,32 +20,9 @@ SILU = mybir.ActivationFunctionType.Silu
 MULT = mybir.AluOpType.mult
 ADD = mybir.AluOpType.add
 
-GROUPS = [256, 256, 256, 256, 256, 128, 128]
-TURN_COPY_ON_VECTOR = (2, 4)
-SHARED_COPY_ON_VECTOR = (1,)
-WORD_RING = 3
-WORDS_ON_GPSIMD = (1, 2, 5)
-PLANES_ON_GPSIMD = (3, 5)
-SHARED_DIRECT = 2
-DIRECT = (3, 4, 5)
-PERMUTE_AHEAD = 1
-W1P_CUT = 6
-MEMSETS = ['w2sp', 'w1pb', 'w1sp', 'w1pa', 'w2p']
-W1_CUTS = (0, 1, 2, 6)
-W2_CUTS = (0, 3, 6)
-WORD_FIRST = True
-SHARED_AT = (7, 7)
-YS_ON_VECTOR = ()
-BYTE_RING = 3
-AHEAD = 1
-Y_COPY_ON_VECTOR = ((0, 512),)
-LOADS = [('s', 'xs'), ('s', ('w1', 0)), ('s', 'w1pa'), ('s', ('w1', 1)), ('s', ('w1', 2)), ('s', ('gate', 1)), ('s', ('w2', 1)), ('s', 'w1sp'), ('a', 'xw'), ('s', 'w2sw'), ('s', ('w2', 0)), ('a', ('pos', 2)), ('s', 'w2p'), ('a', ('gate', 0)), ('s', 'w1sw'), ('s', ('gate', 2)), ('a', ('pos', 0)), ('s', 'w2sp'), ('a', 'w1pb'), ('s', ('pos', 1))]
-LAST_ON_VECTOR = (2, 3)
-YS_BANKS = (4, 3, 6, 5)
-S_BANKS = (0, 7, 3, 4)
-B_BANKS = (2, 0, 2, 6)
-STEPS = [('h', 0), ('G', 0, 2), ('h', 1), ('y', 1, 1), ('G', 0, 0), ('y', 1, 2), ('y', 1, 0), ('G', 1, 2), ('G', 0, 1), ('y', 2, 2), ('G', 1, 0), ('y', 3, 1), ('y', 3, 0), ('y', 2, 1), ('y', 3, 2), ('y', 2, 0), ('ys', 0), ('G', 3, 0), ('G', 3, 1), ('G', 1, 1), ('ys', 1), ('S', 0), ('G', 2, 0), ('ys', 3), ('ys', 2), ('G', 2, 1), ('S', 1), ('B', 0), ('B', 1), ('G', 2, 2), ('S', 3), ('S', 2), ('B', 3), ('B', 2), ('L', 3, 1), ('L', 3, 0), ('F', 3, 1), ('F', 3, 0), ('W', 2)]
-Y0_BANKS = [(0, 512), (512, 1024), (1024, 1408), (1408, 1536)]
+PIECES = (128, 256, 384, 256, 256, 256)
+TURNED = 3
+FIRST_LOAD = 4
 
 
 def tile_moe_shf_mlp_silu_kernel(
@@ -55,7 +32,6 @@ def tile_moe_shf_mlp_silu_kernel(
     nc = tc.nc
     with ExitStack() as ctx:
         keep = ctx.enter_context(tc.tile_pool(name="keep", bufs=1))
-        ring = ctx.enter_context(tc.tile_pool(name="ring", bufs=1))
         psum = ctx.enter_context(tc.psum_pool(name="psum", bufs=1))
 
         def held(shape, dtype, name):
@@ -67,7 +43,8 @@ def tile_moe_shf_mlp_silu_kernel(
         pos_sb = [keep.tile([P, T // 16], U16, name="pos_sb%d" % r) for r in range(TOP)]
         xw = held([P, T], I32, "xw")
         xs = held([P, T // 4], I32, "xs")
-        w1w = held([P, E, 2 * H], U8, "w1w")
+        w1w_a = held([P, FIRST_LOAD, 2 * H], U8, "w1w_a")
+        w1w_b = held([P, E - FIRST_LOAD, 2 * H], U8, "w1w_b")
         w2w = held([P, E, 2 * N], U8, "w2w")
         w1p = held([P, E, H // 4], I32, "w1p")
         w2p = held([P, E, N // 4], I32, "w2p")
@@ -75,306 +52,269 @@ def tile_moe_shf_mlp_silu_kernel(
         w2sw = held([P, N], I32, "w2sw")
         w1sp = held([P, H // 4], I32, "w1sp")
         w2sp = held([P, N // 4], I32, "w2sp")
-        gate_sb = held([P, TOP, T], F32, "gate_sb")
+        gate_sb = [held([P, T], F32, "gate_sb%d" % r) for r in range(TOP)]
         ident = held([P, P], F32, "ident")
         warm = held([P, 8], F32, "warm")
 
-        planes = {"w2p": w2p[:], "w1sp": w1sp[:], "w2sp": w2sp[:], "w1pa": w1p[:, 0:W1P_CUT, :], "w1pb": w1p[:, W1P_CUT:E, :]}
-        for name in MEMSETS:
-            if name != "w1pb" or W1P_CUT < E:
-                nc.vector.memset(planes[name], 0)
+        def w1w(e):
+            return w1w_a[:, e, :] if e < FIRST_LOAD else w1w_b[:, e - FIRST_LOAD, :]
+
+        nc.vector.memset(w1p[:], 0)
+        nc.vector.memset(w1sp[:], 0)
         nc.gpsimd.memset(warm[:], 0.0)
-        nc.scalar.activation(warm[:], warm[:], SILU)
         make_identity(nc, ident[:])
+        nc.gpsimd.memset(w2p[:], 0)
+        nc.gpsimd.memset(w2sp[:], 0)
 
         def load_words(queue, tile_ap, dram):
             queue.dma_start(tile_ap, dram[0].rearrange("p n d -> p (n d)").bitcast(I32))
 
-        def load_experts(queue, tile, dram, lo, hi):
+        def load_experts(queue, tile_ap, dram, lo, hi):
             rows = dram[lo:hi, 0].rearrange("e p n -> p e n")
-            queue.dma_start(tile[:, lo:hi, :].bitcast(I32), rows.bitcast(I32))
+            queue.dma_start(tile_ap.bitcast(I32), rows.bitcast(I32))
 
-        def load_plane(queue, plane, dram):
-            for q in range(4):
-                queue.dma_start(plane[32 * q : 32 * q + 4, :], dram[0, 4 * q : 4 * q + 4, :].bitcast(I32))
+        def load_rows(queue, plane, dram, q):
+            queue.dma_start(plane[32 * q : 32 * q + 4, :], dram[0, 4 * q : 4 * q + 4, :].bitcast(I32))
 
-        def load_planes(queue, plane, dram):
-            for q in range(4):
-                rows = dram[:, 0, 4 * q : 4 * q + 4, :].rearrange("e r n -> r e n")
-                queue.dma_start(plane[32 * q : 32 * q + 4, :, :], rows.bitcast(I32))
+        def load_expert_rows(queue, plane, dram, q):
+            rows = dram[:, 0, 4 * q : 4 * q + 4, :].rearrange("e r n -> r e n")
+            queue.dma_start(plane[32 * q : 32 * q + 4, :, :], rows.bitcast(I32))
+
+        def load_token_rows(queue, q):
+            rows = x_scales[0, 4 * q : 4 * q + 4, :].bitcast(I32)
+            queue.dma_start(xs[32 * q : 32 * q + 32, :], rows.unsqueeze(0).to_broadcast([8, 4, T // 4]))
 
         nc.sync.dma_start(offs_sb[:], offs)
-        queues = {"s": nc.sync, "a": nc.scalar}
-        for qn, what in LOADS:
-            queue = queues[qn]
-            if what == "xs":
-                for q in range(4):
-                    rows = x_scales[0, 4 * q : 4 * q + 4, :].bitcast(I32)
-                    queue.dma_start(xs[32 * q : 32 * q + 32, :], rows.unsqueeze(0).to_broadcast([8, 4, T // 4]))
-            elif what == "xw":
-                load_words(queue, xw[:], x_words)
-            elif what[0] == "w1":
-                load_experts(queue, w1w, w1_words, W1_CUTS[what[1]], W1_CUTS[what[1] + 1])
-            elif what[0] == "w2":
-                load_experts(queue, w2w, w2_words, W2_CUTS[what[1]], W2_CUTS[what[1] + 1])
-            elif what == "w1pa":
-                load_planes(queue, w1p[:, 0:W1P_CUT, :], w1_scales[0:W1P_CUT])
-            elif what == "w1pb":
-                if W1P_CUT < E:
-                    load_planes(queue, w1p[:, W1P_CUT:E, :], w1_scales[W1P_CUT:E])
-            elif what == "w2p":
-                load_planes(queue, w2p[:], w2_scales)
-            elif what == "w1sw":
-                load_words(queue, w1sw[:], w1s_words)
-            elif what == "w2sw":
-                load_words(queue, w2sw[:], w2s_words)
-            elif what == "w1sp":
-                load_plane(queue, w1sp, w1s_scales)
-            elif what == "w2sp":
-                load_plane(queue, w2sp, w2s_scales)
-            elif what[0] == "pos":
-                nc.sync.dma_start(pos_sb[what[1]][:], (pos1, pos2, pos3)[what[1]])
-            elif what[0] == "gate":
-                queue.dma_start(gate_sb[:, what[1], :], gate[what[1]])
+        for q in range(4):
+            load_token_rows(nc.sync if q < 2 else nc.scalar, q)
+        load_words(nc.scalar, xw[:], x_words)
+        nc.scalar.activation(warm[:], warm[:], SILU)
+        load_experts(nc.sync, w1w_a[:], w1_words, 0, FIRST_LOAD)
+        for q in range(4):
+            load_expert_rows(nc.sync if q < 3 else nc.scalar, w1p, w1_scales, q)
+        load_experts(nc.sync, w1w_b[:], w1_words, FIRST_LOAD, E)
+        for q in range(4):
+            load_rows(nc.scalar, w1sp, w1s_scales, q)
+        load_words(nc.sync, w1sw[:], w1s_words)
+        load_experts(nc.sync, w2w[:], w2_words, 0, E)
+        for q in range(4):
+            load_expert_rows(nc.sync, w2p, w2_scales, q)
+        for r, pos in enumerate((pos1, pos2, pos3)):
+            nc.sync.dma_start(pos_sb[r][:], pos)
+            nc.sync.dma_start(gate_sb[r][:], gate[r])
+        load_words(nc.sync, w2sw[:], w2s_words)
+        for q in range(4):
+            load_rows(nc.sync, w2sp, w2s_scales, q)
 
-        first_banks = banks[0:3]
-        turn_banks = banks[3:5]
-        y_banks = banks[5:8]
-        used = {"first": 0, "turn": 0, "y": 0}
+        unit_words, unit_plane = [], []
+        at = 0
+        for g, cols in enumerate(PIECES):
+            picks = offs_sb[:, at // 16 : (at + cols) // 16]
+            xgp = held([P, cols], U8, "xgp%d" % g)
+            xg = held([P, cols], U32, "xg%d" % g)
+            nc.vector.tensor_copy(xgp[:], xs[:].bitcast(U8).indirect(picks))
+            nc.vector.tensor_copy(xg[:], xw[:].bitcast(U32).indirect(picks))
+            for a in range(cols // P):
+                unit_words.append(xg[:, a * P : (a + 1) * P])
+                unit_plane.append(xgp[:, a * P : (a + 1) * P])
+            at = at + cols
 
-        def next_bank(role, ring):
-            bank = ring[used[role] % len(ring)]
-            used[role] = used[role] + 1
-            return bank
+        direct = E - TURNED
+        words_by_t = {}
+        planes_by_t = held([P, direct, H], U8, "planes_by_t")
 
-        def hidden(name, cols, x_codes, x_plane, w_codes, w_plane, copy_on_vector, first_ring):
-            tiles = cols // P
-            turned = next_bank("turn", turn_banks)
-            for a in range(tiles):
-                acc = next_bank("first", first_ring)
-                nc.tensor.matmul_mx(
-                    out=acc[:], lhsT=x_codes[:, a * P : (a + 1) * P].bitcast(FP8X4),
-                    lhsT_scale=x_plane[:, a * P : (a + 1) * P], rhs=w_codes, rhs_scale=w_plane,
-                    start=True, stop=True,
+        def permute_words(e):
+            words = held([P, 2 * H], U8, "w1_words_by_t%d" % e)
+            for b in range(2):
+                nc.gpsimd.tensor_copy(
+                    words[:].rearrange("p (t m b) -> p b t m", t=4, b=2)[:, b],
+                    w1w(e).rearrange("p (m t b) -> p b t m", t=4, b=2)[:, b],
                 )
-                act = held([P, H], BF16, "act_%s_%d" % (name, a))
-                nc.scalar.activation(
-                    act[:].rearrange("s (u p e) -> s u p e", u=2, e=2),
-                    acc[:].rearrange("s (p u e) -> s u p e", u=2, e=2), SILU,
-                )
-                words = act[:].bitcast(F32)
-                for u in range(2):
-                    at = (2 * a + u) * P
-                    nc.tensor.transpose(turned[:, at : at + P], words[:, u * P : (u + 1) * P], ident[:])
-            grouped = held([P, 2 * cols], F32, "grouped_" + name)
-            src = turned[:, 0 : 2 * cols].rearrange("p (a u s) -> p a s u", u=2, s=P)
-            dst = grouped[:].rearrange("p (a s u) -> p a s u", u=2, s=P)
-            if copy_on_vector:
+            words_by_t[e] = words
+
+        permute_words(TURNED)
+        nc.gpsimd.tensor_copy(
+            planes_by_t[:].rearrange("p e (t m) -> p e t m", t=4),
+            w1p[:, TURNED:E, :].bitcast(U8).rearrange("p e (m t) -> p e t m", t=4),
+        )
+        for e in range(TURNED + 1, E):
+            permute_words(e)
+        shared_words = held([P, H], I32, "w1s_words_by_t")
+        shared_plane = held([P, H], U8, "w1s_plane_by_t")
+        nc.gpsimd.tensor_copy(shared_words[:].rearrange("p (t m) -> p t m", t=4), w1sw[:].rearrange("p (m t) -> p t m", t=4))
+        nc.gpsimd.tensor_copy(shared_plane[:].rearrange("p (t m) -> p t m", t=4), w1sp[:].bitcast(U8).rearrange("p (m t) -> p t m", t=4))
+
+        def copy_out(engine, dst, src):
+            if engine is nc.vector:
                 nc.vector.tensor_copy(dst, src)
             else:
                 nc.scalar.copy(dst, src)
-            codes = held([P, cols], U32, "codes_" + name)
-            plane = held([P, cols], U8, "plane_" + name)
-            nc.vector.quantize_mx(out=codes[:].bitcast(FP8X4), scales=plane[:], in_=grouped[:].bitcast(BF16))
-            return codes, plane
 
-        def by_column(engine, dst, src):
-            engine.tensor_copy(dst.rearrange("p (t m) -> p t m", t=4), src.rearrange("p (m t) -> p t m", t=4))
+        def first_turned(acc, turned, a, x_codes, x_plane, e):
+            nc.tensor.matmul_mx(
+                out=acc[:], lhsT=x_codes.bitcast(FP8X4), lhsT_scale=x_plane,
+                rhs=w1w(e).bitcast(FP4X4), rhs_scale=w1p[:, e, :].bitcast(U8), start=True, stop=True,
+            )
+            act = held([P, H], BF16, "act_%d_%d" % (e, a))
+            nc.scalar.activation(
+                act[:].rearrange("s (u p e) -> s u p e", u=2, e=2),
+                acc[:].rearrange("s (p u e) -> s u p e", u=2, e=2), SILU,
+            )
+            words = act[:].bitcast(F32)
+            for u in range(2):
+                col = (2 * a + u) * P
+                nc.tensor.transpose(turned[:, col : col + P], words[:, u * P : (u + 1) * P], ident[:])
 
-        def permuted(e):
-            words = held([P, H], U16, "w1_words_by_t%d" % e)
-            plane = held([P, H], U8, "w1_plane_by_t%d" % e)
-            if e in WORDS_ON_GPSIMD:
-                for b in range(2):
-                    nc.gpsimd.tensor_copy(
-                        words[:].bitcast(U8).rearrange("p (t m b) -> p b t m", t=4, b=2)[:, b],
-                        w1w[:, e, :].rearrange("p (m t b) -> p b t m", t=4, b=2)[:, b],
-                    )
-            else:
-                by_column(nc.vector, words[:], w1w[:, e, :].bitcast(U16))
-            by_column(nc.gpsimd if e in PLANES_ON_GPSIMD else nc.vector, plane[:], w1p[:, e, :].bitcast(U8))
-            return words[:].bitcast(FP4X4), plane
-
-        def hidden_direct(name, cols, x_codes, x_plane, words, plane, first_ring):
-            grouped = held([P, 4 * cols], BF16, "grouped_" + name)
-            for a in range(cols // P):
-                acc = next_bank("first", first_ring)
-                slots = slice(a * P, (a + 1) * P)
-                for t in range(4):
-                    nc.tensor.matmul_mx(
-                        out=acc[:, t * P : (t + 1) * P], lhsT=words[:, t * P : (t + 1) * P],
-                        lhsT_scale=plane[:, t * P : (t + 1) * P], rhs=x_codes[:, slots].bitcast(FP8X4),
-                        rhs_scale=x_plane[:, slots], start=True, stop=True,
-                    )
-                nc.scalar.activation(
-                    grouped[:, a * H : (a + 1) * H].rearrange("p (s t) -> p s t", t=4),
-                    acc[:].rearrange("p (t s) -> p s t", t=4), SILU,
+        def first_direct(acc, dst, x_codes, x_plane, words, plane):
+            for t in range(4):
+                nc.tensor.matmul_mx(
+                    out=acc[:, t * P : (t + 1) * P], lhsT=words[:, t * P : (t + 1) * P],
+                    lhsT_scale=plane[:, t * P : (t + 1) * P], rhs=x_codes.bitcast(FP8X4),
+                    rhs_scale=x_plane, start=True, stop=True,
                 )
-            codes = held([P, cols], U32, "codes_" + name)
-            scales = held([P, cols], U8, "plane_" + name)
-            nc.vector.quantize_mx(out=codes[:].bitcast(FP8X4), scales=scales[:], in_=grouped[:])
-            return codes, scales
+            nc.scalar.activation(
+                dst.rearrange("p (s t) -> p s t", t=4), acc[:].rearrange("p (t s) -> p s t", t=4), SILU,
+            )
+
+        def quantise(codes, plane, grouped, lo, hi):
+            nc.vector.quantize_mx(out=codes[:, lo:hi].bitcast(FP8X4), scales=plane[:, lo:hi], in_=grouped[:, 4 * lo : 4 * hi])
 
         y_sb = [held([P, SLOTS], F32, "y_sb%d" % j) for j in range(N // P)]
-        starts = [sum(GROUPS[:g]) for g in range(len(GROUPS))]
+        h_codes = [held([P, C], U32, "h_codes%d" % e) for e in range(E)]
+        h_plane = [held([P, C], U8, "h_plane%d" % e) for e in range(E)]
 
-        def gather(g):
-            cols = GROUPS[g]
-            picks = offs_sb[:, starts[g] // 16 : (starts[g] + cols) // 16]
-            xg = ring.tile([P, cols], U32, name="xg", bufs=WORD_RING, align_bytes=64)
-            xgp = ring.tile([P, cols], U8, name="xgp", bufs=BYTE_RING, align_bytes=64)
-            if WORD_FIRST:
-                nc.vector.tensor_copy(xg[:], xw[:].bitcast(U32).indirect(picks))
-            nc.vector.tensor_copy(xgp[:], xs[:].bitcast(U8).indirect(picks))
-            if not WORD_FIRST:
-                nc.vector.tensor_copy(xg[:], xw[:].bitcast(U32).indirect(picks))
-            return xg, xgp
+        def second(j, lo, hi, bank, engine):
+            for e in range(lo // C, (hi + C - 1) // C):
+                a, b = max(lo, e * C), min(hi, (e + 1) * C)
+                nc.tensor.matmul_mx(
+                    out=bank[:, a - lo : b - lo],
+                    lhsT=w2w[:, e, 2 * j * P : 2 * (j + 1) * P].bitcast(FP4X4),
+                    lhsT_scale=w2p[:, e, :].bitcast(U8)[:, j * P : (j + 1) * P],
+                    rhs=h_codes[e][:, a - e * C : b - e * C].bitcast(FP8X4), rhs_scale=h_plane[e][:, a - e * C : b - e * C],
+                    start=True, stop=True,
+                )
+            copy_out(engine, y_sb[j][:, lo:hi], bank[:, 0 : hi - lo])
 
-        h = []
-
-        def second(j, lo, hi):
-            bank = next_bank("y", y_banks)
-            for g, cols in enumerate(GROUPS):
-                if lo <= starts[g] < hi:
-                    e = starts[g] // C
-                    nc.tensor.matmul_mx(
-                        out=bank[:, starts[g] - lo : starts[g] - lo + cols],
-                        lhsT=w2w[:, e, 2 * j * P : 2 * (j + 1) * P].bitcast(FP4X4),
-                        lhsT_scale=w2p[:, e, :].bitcast(U8)[:, j * P : (j + 1) * P],
-                        rhs=h[g][0][:].bitcast(FP8X4), rhs_scale=h[g][1][:], start=True, stop=True,
+        pending = []
+        for e in range(E):
+            grouped = held([P, 4 * C], BF16, "grouped%d" % e)
+            for a in range(2):
+                u = 2 * e + a
+                acc = banks[u % 3]
+                if e < TURNED:
+                    first_turned(acc, banks[3 + e], a, unit_words[u], unit_plane[u], e)
+                else:
+                    first_direct(
+                        acc, grouped[:, a * H : (a + 1) * H], unit_words[u], unit_plane[u],
+                        words_by_t[e][:].bitcast(FP4X4), planes_by_t[:, e - TURNED, :],
                     )
-            if (j, lo) in Y_COPY_ON_VECTOR:
-                nc.vector.tensor_copy(y_sb[j][:, lo:hi], bank[:, 0 : hi - lo])
-            else:
-                nc.scalar.copy(y_sb[j][:, lo:hi], bank[:, 0 : hi - lo])
+                if a == 0:
+                    for step in pending:
+                        step()
+                    pending = []
+                if e == E - 1:
+                    quantise(h_codes[e], h_plane[e], grouped, a * P, (a + 1) * P)
 
-        hs, by_t = {}, {}
+            def close(e=e, grouped=grouped):
+                if e < TURNED:
+                    src = banks[3 + e][:].rearrange("p (a u s) -> p a s u", u=2, s=P)
+                    dst = grouped[:].bitcast(F32).rearrange("p (a s u) -> p a s u", u=2, s=P)
+                    copy_out(nc.vector if e == TURNED - 1 else nc.scalar, dst, src)
+                quantise(h_codes[e], h_plane[e], grouped, 0, C)
 
-        def shared_first(i, ring_banks):
-            cols = slice(i * 256, (i + 1) * 256)
-            if SHARED_DIRECT:
-                if "s" not in by_t:
-                    words = held([P, H], I32, "w1s_words_by_t")
-                    plane = held([P, H], U8, "w1s_plane_by_t")
-                    by_column(nc.gpsimd if SHARED_DIRECT == 2 else nc.vector, words[:], w1sw[:])
-                    by_column(nc.gpsimd if SHARED_DIRECT == 2 else nc.vector, plane[:], w1sp[:].bitcast(U8))
-                    by_t["s"] = (words[:].bitcast(FP8X4), plane)
-                hs[i] = hidden_direct("s%d" % i, 256, xw[:, cols], xs[:].bitcast(U8)[:, cols], *by_t["s"], ring_banks)
-                return
-            hs[i] = hidden(
-                "s%d" % i, 256, xw[:, cols], xs[:].bitcast(U8)[:, cols],
-                w1sw[:].bitcast(FP8X4), w1sp[:].bitcast(U8), i in SHARED_COPY_ON_VECTOR, ring_banks,
-            )
+            if e < E - 1:
+                pending.append(close)
 
-        gathered = [gather(g) for g in range(AHEAD)]
-        for g, cols in enumerate(GROUPS):
-            e = starts[g] // C
-            for i in range(2):
-                if SHARED_AT[i] == g:
-                    shared_first(i, first_banks)
-            if g + AHEAD < len(GROUPS):
-                gathered.append(gather(g + AHEAD))
-            for later in DIRECT:
-                if max(later - PERMUTE_AHEAD, 0) == e and later not in by_t:
-                    by_t[later] = permuted(later)
-            if e in DIRECT:
-                h.append(hidden_direct("g%d" % g, cols, gathered[g][0][:], gathered[g][1][:], *by_t[e], first_banks))
-            else:
-                h.append(hidden(
-                    "g%d" % g, cols, gathered[g][0][:], gathered[g][1][:],
-                    w1w[:, e, :].bitcast(FP4X4), w1p[:, e, :].bitcast(U8), g in TURN_COPY_ON_VECTOR, first_banks,
-                ))
-            for lo, hi in Y0_BANKS:
-                if hi == starts[g] + cols:
-                    second(0, lo, hi)
-
-        def shared_second(b, bank):
-            codes, plane = hs[b // 2]
-            cols = slice((b % 2) * P, (b % 2 + 1) * P)
-            nc.tensor.matmul_mx(
-                out=bank[:], lhsT=codes[:, cols].bitcast(FP8X4), lhsT_scale=plane[:, cols],
-                rhs=w2sw[:].bitcast(FP8X4), rhs_scale=w2sp[:].bitcast(U8), start=True, stop=True,
-            )
-            ys = held([P, N], F32, "ys%d" % b)
-            if b in YS_ON_VECTOR:
-                nc.vector.tensor_copy(ys[:], bank[:])
-            else:
-                nc.scalar.copy(ys[:], bank[:])
-            return ys
-
-        def fetch(j, r):
-            term = held([P, T], F32, "term%d_%d" % (j, r))
-            nc.vector.tensor_tensor(term[:], y_sb[j][:].indirect(pos_sb[r][:]), gate_sb[:, r, :], MULT)
-            return term
+        second(0, 0, 512, banks[5], nc.vector)
+        second(0, 512, 1024, banks[3], nc.scalar)
+        second(0, 1024, 1408, banks[4], nc.scalar)
+        second(0, 1408, 1536, banks[6], nc.vector)
 
         blocks = T // P
+        terms = {}
 
-        def turn_add(bank, sources):
-            for i, source in enumerate(sources):
-                for b in range(blocks):
-                    nc.tensor.matmul(
-                        bank[:, b * P : (b + 1) * P], lhsT=source[b], rhs=ident[:],
-                        start=(i == 0 and b == 0), stop=(i == len(sources) - 1 and b == blocks - 1),
-                        is_transpose=True,
-                    )
+        def fetch(j, r, term=None):
+            if term is None:
+                term = held([P, T], F32, "term%d_%d" % (j, r))
+            nc.vector.tensor_tensor(term[:], y_sb[j][:].indirect(pos_sb[r][:]), gate_sb[r][:], MULT)
+            terms[j, r] = term
 
-        def cut(tile):
-            return [tile[:, b * P : (b + 1) * P] for b in range(blocks)]
+        def turn_add(bank, source, opens, closes):
+            for b in range(blocks):
+                nc.tensor.matmul(
+                    bank[:, b * P : (b + 1) * P], lhsT=source[:, b * P : (b + 1) * P], rhs=ident[:],
+                    start=(opens and b == 0), stop=(closes and b == blocks - 1), is_transpose=True,
+                )
 
-        def add_terms(j, terms, bank):
-            turn_add(bank, [cut(term) for term in terms])
+        def flip(j, count, bank):
+            for r in range(count):
+                turn_add(bank, terms[j, r], r == 0, r == count - 1)
             flipped = held([P, T], F32, "flipped%d" % j)
             nc.scalar.copy(flipped[:], bank[:])
             return flipped
 
-        def turn_back(j, flipped, bank):
-            turn_add(bank, [[ys_t[b][:, j * P : (j + 1) * P] for b in range(blocks)], cut(flipped)])
-            return bank
+        hs_grouped = held([P, 4 * T], BF16, "hs_grouped")
+        hs_codes = held([P, T], U32, "hs_codes")
+        hs_plane = held([P, T], U8, "hs_plane")
 
-        def finish(j, back, last):
+        def shared_second(j, bank):
+            for b in range(blocks):
+                nc.tensor.matmul_mx(
+                    out=bank[:, b * P : (b + 1) * P], lhsT=hs_codes[:, b * P : (b + 1) * P].bitcast(FP8X4),
+                    lhsT_scale=hs_plane[:, b * P : (b + 1) * P], rhs=w2sw[:, j * P : (j + 1) * P].bitcast(FP8X4),
+                    rhs_scale=w2sp[:].bitcast(U8)[:, j * P : (j + 1) * P], start=True, stop=True,
+                )
+            ys = held([P, T], F32, "ys%d" % j)
+            nc.scalar.copy(ys[:], bank[:])
+            return ys
+
+        def back(ys, flipped, bank):
+            turn_add(bank, ys, True, False)
+            turn_add(bank, flipped, False, True)
+
+        def finish(j, bank, last):
             res = held([P, T], F32, "res%d" % j)
             if last is None:
-                nc.scalar.copy(res[:], back[:])
+                nc.scalar.copy(res[:], bank[:])
             else:
-                nc.vector.tensor_tensor(res[:], back[:], last[:], ADD)
+                nc.vector.tensor_tensor(res[:], bank[:], last[:], ADD)
             nc.sync.dma_start(out[j * P : (j + 1) * P, :], res[:])
 
-        half = T // 2
-        ys_t, terms, flips, backs = {}, {}, {}, {}
+        def second_tile(j, three):
+            for i in range(3):
+                second(j, i * 512, (i + 1) * 512, banks[three[i]], nc.scalar)
 
-        def last_half(j, i):
-            picks = pos_sb[TOP - 1][:, i * half // 16 : (i + 1) * half // 16]
-            term = held([P, half], F32, "last%d_%d" % (j, i))
-            nc.vector.tensor_tensor(term[:], y_sb[j][:].indirect(picks), gate_sb[:, TOP - 1, i * half : (i + 1) * half], MULT)
-            return term
-
-        for step in STEPS:
-            kind = step[0]
-            if kind == "y":
-                second(step[1], step[2] * 512, (step[2] + 1) * 512)
-            elif kind == "h":
-                if SHARED_AT[step[1]] >= len(GROUPS):
-                    shared_first(step[1], banks[0:2])
-            elif kind == "ys":
-                ys_t[step[1]] = shared_second(step[1], banks[YS_BANKS[step[1]]])
-            elif kind == "G":
-                terms[step[1], step[2]] = fetch(step[1], step[2])
-            elif kind == "L":
-                terms[step[1], "L", step[2]] = last_half(step[1], step[2])
-            elif kind == "S":
-                j = step[1]
-                flips[j] = add_terms(j, [terms[j, r] for r in range(TOP if j not in LAST_ON_VECTOR else TOP - 1)], banks[S_BANKS[j]])
-            elif kind == "B":
-                j = step[1]
-                backs[j] = turn_back(j, flips[j], banks[B_BANKS[j]])
-                if j not in LAST_ON_VECTOR:
-                    finish(j, backs[j], None)
-            elif kind == "F":
-                j, i = step[1], step[2]
-                cols = slice(i * half, (i + 1) * half)
-                res = held([P, half], F32, "res%d_%d" % (j, i))
-                nc.vector.tensor_tensor(res[:], backs[j][:, cols], terms[j, "L", i][:], ADD)
-                nc.sync.dma_start(out[j * P : (j + 1) * P, cols], res[:])
-            elif kind == "W":
-                if step[1] in LAST_ON_VECTOR:
-                    finish(step[1], backs[step[1]], terms[step[1], TOP - 1])
+        for r in range(TOP):
+            fetch(0, r)
+        for b, bank in enumerate((0, 1, 2, 7)):
+            first_direct(
+                banks[bank], hs_grouped[:, b * H : (b + 1) * H], xw[:, b * P : (b + 1) * P],
+                xs[:].bitcast(U8)[:, b * P : (b + 1) * P], shared_words[:].bitcast(FP8X4), shared_plane[:],
+            )
+        quantise(hs_codes, hs_plane, hs_grouped, 0, T)
+        second_tile(1, (5, 3, 4))
+        for r in range(TOP):
+            fetch(1, r)
+        second_tile(2, (6, 0, 1))
+        for r in range(TOP - 1):
+            fetch(2, r)
+        flipped0 = flip(0, TOP, banks[5])
+        ys0 = shared_second(0, banks[2])
+        second_tile(3, (7, 3, 4))
+        for r in range(TOP):
+            fetch(3, r)
+        ys1 = shared_second(1, banks[0])
+        back(ys0, flipped0, banks[6])
+        finish(0, banks[6], None)
+        flipped1 = flip(1, TOP, banks[7])
+        ys2 = shared_second(2, banks[1])
+        ys3 = shared_second(3, banks[2])
+        back(ys1, flipped1, banks[5])
+        finish(1, banks[5], None)
+        flipped2 = flip(2, TOP - 1, banks[6])
+        flipped3 = flip(3, TOP - 1, banks[1])
+        fetch(2, TOP - 1, terms[3, 0])
+        back(ys2, flipped2, banks[3])
+        back(ys3, flipped3, banks[4])
+        finish(2, banks[3], terms[2, TOP - 1])
+        finish(3, banks[4], terms[3, TOP - 1])

@@ -130,15 +130,20 @@ def tile_moe_shf_mlp_silu_kernel(
                     words[:].rearrange("p (t m b) -> p b t m", t=4, b=2)[:, b],
                     w1w(e).rearrange("p (m t b) -> p b t m", t=4, b=2)[:, b],
                 )
-            words_by_t[e] = words
+            words_by_t[e] = words[:]
 
         permute_words(TURNED)
         nc.gpsimd.tensor_copy(
             planes_by_t[:].rearrange("p e (t m) -> p e t m", t=4),
             w1p[:, TURNED:E, :].bitcast(U8).rearrange("p e (m t) -> p e t m", t=4),
         )
-        for e in range(TURNED + 1, E):
-            permute_words(e)
+        last_words = held([P, E - FIRST_LOAD, 2 * H], U8, "w1_words_by_t_last")
+        nc.vector.tensor_copy(
+            last_words[:].bitcast(U16).rearrange("p e (t m) -> p e t m", t=4),
+            w1w_b[:].bitcast(U16).rearrange("p e (m t) -> p e t m", t=4),
+        )
+        for e in range(FIRST_LOAD, E):
+            words_by_t[e] = last_words[:, e - FIRST_LOAD, :]
         shared_words = held([P, H], I32, "w1s_words_by_t")
         shared_plane = held([P, H], U8, "w1s_plane_by_t")
         nc.gpsimd.tensor_copy(shared_words[:].rearrange("p (t m) -> p t m", t=4), w1sw[:].rearrange("p (m t) -> p t m", t=4))
@@ -150,16 +155,19 @@ def tile_moe_shf_mlp_silu_kernel(
             else:
                 nc.scalar.copy(dst, src)
 
-        def first_turned(acc, turned, a, x_codes, x_plane, e):
+        def first_turned(acc, u, x_codes, x_plane, e):
             nc.tensor.matmul_mx(
                 out=acc[:], lhsT=x_codes.bitcast(FP8X4), lhsT_scale=x_plane,
                 rhs=w1w(e).bitcast(FP4X4), rhs_scale=w1p[:, e, :].bitcast(U8), start=True, stop=True,
             )
-            act = held([P, H], BF16, "act_%d_%d" % (e, a))
+            act = held([P, H], BF16, "act_%d" % u)
             nc.scalar.activation(
                 act[:].rearrange("s (u p e) -> s u p e", u=2, e=2),
                 acc[:].rearrange("s (p u e) -> s u p e", u=2, e=2), SILU,
             )
+            return act
+
+        def turn(turned, a, act):
             words = act[:].bitcast(F32)
             for u in range(2):
                 col = (2 * a + u) * P
@@ -195,63 +203,57 @@ def tile_moe_shf_mlp_silu_kernel(
                 )
             copy_out(engine, y_sb[j][:, lo:hi], bank[:, 0 : hi - lo])
 
-        pending = []
-        for e in range(E):
-            grouped = held([P, 4 * C], BF16, "grouped%d" % e)
+        grouped = [held([P, 4 * C], BF16, "grouped%d" % e) for e in range(E)]
+        first_ring = (0, 1, 2, 6, 7)
+        acts = {}
+        for u in range(2 * TURNED):
+            acts[u] = first_turned(banks[first_ring[u % 5]], u, unit_words[u], unit_plane[u], u // 2)
+        for e in range(TURNED):
+            for a in range(2):
+                turn(banks[3 + e], a, acts[2 * e + a])
+            src = banks[3 + e][:].rearrange("p (a u s) -> p a s u", u=2, s=P)
+            dst = grouped[e][:].bitcast(F32).rearrange("p (a s u) -> p a s u", u=2, s=P)
+            copy_out(nc.vector if e == TURNED - 1 else nc.scalar, dst, src)
+        for e in range(TURNED):
+            quantise(h_codes[e], h_plane[e], grouped[e], 0, C)
+        for e in range(TURNED, E):
             for a in range(2):
                 u = 2 * e + a
-                acc = banks[u % 3]
-                if e < TURNED:
-                    first_turned(acc, banks[3 + e], a, unit_words[u], unit_plane[u], e)
-                else:
-                    first_direct(
-                        acc, grouped[:, a * H : (a + 1) * H], unit_words[u], unit_plane[u],
-                        words_by_t[e][:].bitcast(FP4X4), planes_by_t[:, e - TURNED, :],
-                    )
-                if a == 0:
-                    for step in pending:
-                        step()
-                    pending = []
+                first_direct(
+                    banks[first_ring[u % 5]], grouped[e][:, a * H : (a + 1) * H], unit_words[u], unit_plane[u],
+                    words_by_t[e].bitcast(FP4X4), planes_by_t[:, e - TURNED, :],
+                )
                 if e == E - 1:
-                    quantise(h_codes[e], h_plane[e], grouped, a * P, (a + 1) * P)
-
-            def close(e=e, grouped=grouped):
-                if e < TURNED:
-                    src = banks[3 + e][:].rearrange("p (a u s) -> p a s u", u=2, s=P)
-                    dst = grouped[:].bitcast(F32).rearrange("p (a s u) -> p a s u", u=2, s=P)
-                    copy_out(nc.vector if e == TURNED - 1 else nc.scalar, dst, src)
-                quantise(h_codes[e], h_plane[e], grouped, 0, C)
-
+                    quantise(h_codes[e], h_plane[e], grouped[e], a * P, (a + 1) * P)
             if e < E - 1:
-                pending.append(close)
+                quantise(h_codes[e], h_plane[e], grouped[e], 0, C)
 
         second(0, 0, 512, banks[5], nc.vector)
-        second(0, 512, 1024, banks[3], nc.scalar)
-        second(0, 1024, 1408, banks[4], nc.scalar)
-        second(0, 1408, 1536, banks[6], nc.vector)
+        second(0, 512, 1024, banks[0], nc.scalar)
+        second(0, 1024, 1408, banks[3], nc.scalar)
+        second(0, 1408, 1536, banks[4], nc.vector)
 
         blocks = T // P
-        terms = {}
+        terms = {(j, r): held([P, T], F32, "term%d_%d" % (j, r)) for j in range(N // P) for r in range(TOP)}
 
-        def fetch(j, r, term=None):
-            if term is None:
-                term = held([P, T], F32, "term%d_%d" % (j, r))
-            nc.vector.tensor_tensor(term[:], y_sb[j][:].indirect(pos_sb[r][:]), gate_sb[r][:], MULT)
-            terms[j, r] = term
+        def fetch(j, r, lo=0, hi=T):
+            picks = pos_sb[r][:, lo // 16 : hi // 16]
+            nc.vector.tensor_tensor(terms[j, r][:, lo:hi], y_sb[j][:].indirect(picks), gate_sb[r][:, lo:hi], MULT)
 
-        def turn_add(bank, source, opens, closes):
-            for b in range(blocks):
+        def turn_add(bank, source, opens, closes, lo=0, hi=T):
+            for at in range(lo, hi, P):
                 nc.tensor.matmul(
-                    bank[:, b * P : (b + 1) * P], lhsT=source[:, b * P : (b + 1) * P], rhs=ident[:],
-                    start=(opens and b == 0), stop=(closes and b == blocks - 1), is_transpose=True,
+                    bank[:, at - lo : at - lo + P], lhsT=source[:, at : at + P], rhs=ident[:],
+                    start=(opens and at == lo), stop=(closes and at + P == hi), is_transpose=True,
                 )
 
-        def flip(j, count, bank):
-            for r in range(count):
-                turn_add(bank, terms[j, r], r == 0, r == count - 1)
-            flipped = held([P, T], F32, "flipped%d" % j)
-            nc.scalar.copy(flipped[:], bank[:])
-            return flipped
+        flipped = [held([P, T], F32, "flipped%d" % j) for j in range(N // P)]
+        res = [held([P, T], F32, "res%d" % j) for j in range(N // P)]
+
+        def flip(j, bank):
+            for r in range(TOP):
+                turn_add(bank, terms[j, r], r == 0, r == TOP - 1)
+            nc.scalar.copy(flipped[j][:], bank[:])
 
         hs_grouped = held([P, 4 * T], BF16, "hs_grouped")
         hs_codes = held([P, T], U32, "hs_codes")
@@ -268,17 +270,11 @@ def tile_moe_shf_mlp_silu_kernel(
             nc.scalar.copy(ys[:], bank[:])
             return ys
 
-        def back(ys, flipped, bank):
+        def finish(j, ys, bank):
             turn_add(bank, ys, True, False)
-            turn_add(bank, flipped, False, True)
-
-        def finish(j, bank, last):
-            res = held([P, T], F32, "res%d" % j)
-            if last is None:
-                nc.scalar.copy(res[:], bank[:])
-            else:
-                nc.vector.tensor_tensor(res[:], bank[:], last[:], ADD)
-            nc.sync.dma_start(out[j * P : (j + 1) * P, :], res[:])
+            turn_add(bank, flipped[j], False, True)
+            nc.scalar.copy(res[j][:], bank[:])
+            nc.sync.dma_start(out[j * P : (j + 1) * P, :], res[j][:])
 
         def second_tile(j, three):
             for i in range(3):
@@ -286,35 +282,46 @@ def tile_moe_shf_mlp_silu_kernel(
 
         for r in range(TOP):
             fetch(0, r)
-        for b, bank in enumerate((0, 1, 2, 7)):
+        for b, bank in enumerate((2, 6, 7, 1)):
             first_direct(
                 banks[bank], hs_grouped[:, b * H : (b + 1) * H], xw[:, b * P : (b + 1) * P],
                 xs[:].bitcast(U8)[:, b * P : (b + 1) * P], shared_words[:].bitcast(FP8X4), shared_plane[:],
             )
         quantise(hs_codes, hs_plane, hs_grouped, 0, T)
-        second_tile(1, (5, 3, 4))
+        second_tile(1, (5, 0, 3))
         for r in range(TOP):
             fetch(1, r)
-        second_tile(2, (6, 0, 1))
-        for r in range(TOP - 1):
-            fetch(2, r)
-        flipped0 = flip(0, TOP, banks[5])
-        ys0 = shared_second(0, banks[2])
-        second_tile(3, (7, 3, 4))
+        second_tile(2, (4, 2, 6))
         for r in range(TOP):
-            fetch(3, r)
-        ys1 = shared_second(1, banks[0])
-        back(ys0, flipped0, banks[6])
-        finish(0, banks[6], None)
-        flipped1 = flip(1, TOP, banks[7])
-        ys2 = shared_second(2, banks[1])
-        ys3 = shared_second(3, banks[2])
-        back(ys1, flipped1, banks[5])
-        finish(1, banks[5], None)
-        flipped2 = flip(2, TOP - 1, banks[6])
-        flipped3 = flip(3, TOP - 1, banks[1])
-        fetch(2, TOP - 1, terms[3, 0])
-        back(ys2, flipped2, banks[3])
-        back(ys3, flipped3, banks[4])
-        finish(2, banks[3], terms[2, TOP - 1])
-        finish(3, banks[4], terms[3, TOP - 1])
+            fetch(2, r)
+        flip(0, banks[7])
+        ys0 = shared_second(0, banks[1])
+        second_tile(3, (5, 0, 3))
+        last = N // P - 1
+        halves = ((0, T // 2), (T // 2, T))
+        fetch(last, 0)
+        for r in range(1, TOP):
+            for lo, hi in halves:
+                fetch(last, r, lo, hi)
+        ys1 = shared_second(1, banks[4])
+        finish(0, ys0, banks[2])
+        flip(1, banks[6])
+        ys2 = shared_second(2, banks[7])
+        ys3 = shared_second(3, banks[1])
+        finish(1, ys1, banks[5])
+        back_banks = (banks[0], banks[3])
+        for (lo, hi), bank in zip(halves, back_banks):
+            turn_add(bank, ys3, True, False, lo, hi)
+        flip(2, banks[4])
+        flip_banks = (banks[2], banks[6])
+        for (lo, hi), bank in zip(halves, flip_banks):
+            turn_add(bank, terms[last, 0], True, False, lo, hi)
+        finish(2, ys2, banks[7])
+        for (lo, hi), bank in zip(halves, flip_banks):
+            turn_add(bank, terms[last, 1], False, True, lo, hi)
+            nc.scalar.copy(flipped[last][:, lo:hi], bank[:, 0 : hi - lo])
+        for (lo, hi), bank in zip(halves, back_banks):
+            turn_add(bank, flipped[last], False, True, lo, hi)
+        for (lo, hi), bank in zip(halves, back_banks):
+            nc.vector.tensor_tensor(res[last][:, lo:hi], bank[:, 0 : hi - lo], terms[last, TOP - 1][:, lo:hi], ADD)
+            nc.sync.dma_start(out[last * P : (last + 1) * P, lo:hi], res[last][:, lo:hi])

@@ -20,7 +20,8 @@ SILU = mybir.ActivationFunctionType.Silu
 MULT = mybir.AluOpType.mult
 ADD = mybir.AluOpType.add
 
-PIECES = (128, 256, 384, 256, 256, 256)
+BYTE_PIECES = (128, 128, 256, 256, 384, 384)
+WORD_PIECE = 384
 TURNED = 3
 FIRST_LOAD = 4
 
@@ -34,8 +35,8 @@ def tile_moe_shf_mlp_silu_kernel(
         keep = ctx.enter_context(tc.tile_pool(name="keep", bufs=1))
         psum = ctx.enter_context(tc.psum_pool(name="psum", bufs=1))
 
-        def held(shape, dtype, name):
-            return keep.tile(shape, dtype, name=name, align_bytes=64)
+        def held(shape, dtype, name, tag=""):
+            return keep.tile(shape, dtype, name=name, tag=tag, align_bytes=64)
 
         banks = [psum.tile([P, 512], F32, name="bank%d" % b) for b in range(8)]
 
@@ -44,7 +45,7 @@ def tile_moe_shf_mlp_silu_kernel(
         xw = held([P, T], I32, "xw")
         xs = held([P, T // 4], I32, "xs")
         w1w_a = held([P, FIRST_LOAD, 2 * H], U8, "w1w_a")
-        w1w_b = held([P, E - FIRST_LOAD, 2 * H], U8, "w1w_b")
+        w1w_b = held([P, E - FIRST_LOAD, 2 * H], U8, "w1w_b", "late")
         w2w = held([P, E, 2 * N], U8, "w2w")
         w1p = held([P, E, H // 4], I32, "w1p")
         w2p = held([P, E, N // 4], I32, "w2p")
@@ -85,9 +86,9 @@ def tile_moe_shf_mlp_silu_kernel(
             queue.dma_start(xs[32 * q : 32 * q + 32, :], rows.unsqueeze(0).to_broadcast([8, 4, T // 4]))
 
         nc.sync.dma_start(offs_sb[:], offs)
+        load_words(nc.sync, xw[:], x_words)
         for q in range(4):
-            load_token_rows(nc.sync if q < 2 else nc.scalar, q)
-        load_words(nc.scalar, xw[:], x_words)
+            load_token_rows(nc.sync if q < 1 else nc.scalar, q)
         nc.scalar.activation(warm[:], warm[:], SILU)
         load_experts(nc.sync, w1w_a[:], w1_words, 0, FIRST_LOAD)
         for q in range(4):
@@ -106,18 +107,18 @@ def tile_moe_shf_mlp_silu_kernel(
         for q in range(4):
             load_rows(nc.sync, w2sp, w2s_scales, q)
 
+        def gather(picked, window, at):
+            cols = picked.shape[1]
+            nc.vector.tensor_copy(picked, window.indirect(offs_sb[:, at // 16 : (at + cols) // 16]))
+            return [picked[:, a : a + P] for a in range(0, cols, P)]
+
         unit_words, unit_plane = [], []
-        at = 0
-        for g, cols in enumerate(PIECES):
-            picks = offs_sb[:, at // 16 : (at + cols) // 16]
+        for g in range(2):
+            xg = held([P, WORD_PIECE], U32, "xg%d" % g)
+            unit_words.extend(gather(xg[:], xw[:].bitcast(U32), g * WORD_PIECE))
+        for g, cols in enumerate(BYTE_PIECES):
             xgp = held([P, cols], U8, "xgp%d" % g)
-            xg = held([P, cols], U32, "xg%d" % g)
-            nc.vector.tensor_copy(xgp[:], xs[:].bitcast(U8).indirect(picks))
-            nc.vector.tensor_copy(xg[:], xw[:].bitcast(U32).indirect(picks))
-            for a in range(cols // P):
-                unit_words.append(xg[:, a * P : (a + 1) * P])
-                unit_plane.append(xgp[:, a * P : (a + 1) * P])
-            at = at + cols
+            unit_plane.extend(gather(xgp[:], xs[:].bitcast(U8), sum(BYTE_PIECES[:g])))
 
         direct = E - TURNED
         words_by_t = {}
@@ -144,6 +145,9 @@ def tile_moe_shf_mlp_silu_kernel(
         )
         for e in range(FIRST_LOAD, E):
             words_by_t[e] = last_words[:, e - FIRST_LOAD, :]
+        xg_late = held([P, 2 * WORD_PIECE], U32, "xg_late", "late")
+        for g in range(2):
+            unit_words.extend(gather(xg_late[:, g * WORD_PIECE : (g + 1) * WORD_PIECE], xw[:].bitcast(U32), (2 + g) * WORD_PIECE))
         shared_words = held([P, H], I32, "w1s_words_by_t")
         shared_plane = held([P, H], U8, "w1s_plane_by_t")
         nc.gpsimd.tensor_copy(shared_words[:].rearrange("p (t m) -> p t m", t=4), w1sw[:].rearrange("p (m t) -> p t m", t=4))
@@ -213,7 +217,7 @@ def tile_moe_shf_mlp_silu_kernel(
                 turn(banks[3 + e], a, acts[2 * e + a])
             src = banks[3 + e][:].rearrange("p (a u s) -> p a s u", u=2, s=P)
             dst = grouped[e][:].bitcast(F32).rearrange("p (a s u) -> p a s u", u=2, s=P)
-            copy_out(nc.vector if e == TURNED - 1 else nc.scalar, dst, src)
+            copy_out(nc.scalar if e == 0 else nc.vector, dst, src)
         for e in range(TURNED):
             quantise(h_codes[e], h_plane[e], grouped[e], 0, C)
         for e in range(TURNED, E):

@@ -45,7 +45,7 @@ def tile_moe_shf_mlp_silu_kernel(
         xw = held([P, T], I32, "xw")
         xs = held([P, T // 4], I32, "xs")
         w1w_a = held([P, FIRST_LOAD, 2 * H], U8, "w1w_a")
-        w1w_b = held([P, E - FIRST_LOAD, 2 * H], U8, "w1w_b", "late")
+        w1w_b = held([P, E - FIRST_LOAD, 2 * H], U8, "w1w_b")
         w2w = held([P, E, 2 * N], U8, "w2w")
         w1p = held([P, E, H // 4], I32, "w1p")
         w2p = held([P, E, N // 4], I32, "w2p")
@@ -114,9 +114,9 @@ def tile_moe_shf_mlp_silu_kernel(
 
         unit_words, unit_plane = [], []
         for g in range(2):
-            xg = held([P, WORD_PIECE], U32, "xg%d" % g)
+            xg = held([P, WORD_PIECE], U32, "xg%d" % g, "early%d" % g)
             unit_words.extend(gather(xg[:], xw[:].bitcast(U32), g * WORD_PIECE))
-        for g, cols in enumerate(BYTE_PIECES):
+        for g, cols in enumerate(BYTE_PIECES[:-1]):
             xgp = held([P, cols], U8, "xgp%d" % g)
             unit_plane.extend(gather(xgp[:], xs[:].bitcast(U8), sum(BYTE_PIECES[:g])))
 
@@ -125,29 +125,19 @@ def tile_moe_shf_mlp_silu_kernel(
         planes_by_t = held([P, direct, H], U8, "planes_by_t")
 
         def permute_words(e):
-            words = held([P, 2 * H], U8, "w1_words_by_t%d" % e)
-            for b in range(2):
-                nc.gpsimd.tensor_copy(
-                    words[:].rearrange("p (t m b) -> p b t m", t=4, b=2)[:, b],
-                    w1w(e).rearrange("p (m t b) -> p b t m", t=4, b=2)[:, b],
-                )
-            words_by_t[e] = words[:]
+            words = held([P, H], U16, "w1_words_by_t%d" % e)
+            nc.gpsimd.tensor_copy(
+                words[:].rearrange("p (t m) -> p t m", t=4), w1w(e).bitcast(U16).rearrange("p (m t) -> p t m", t=4),
+            )
+            words_by_t[e] = words[:].bitcast(U8)
 
         permute_words(TURNED)
         nc.gpsimd.tensor_copy(
             planes_by_t[:].rearrange("p e (t m) -> p e t m", t=4),
             w1p[:, TURNED:E, :].bitcast(U8).rearrange("p e (m t) -> p e t m", t=4),
         )
-        last_words = held([P, E - FIRST_LOAD, 2 * H], U8, "w1_words_by_t_last")
-        nc.vector.tensor_copy(
-            last_words[:].bitcast(U16).rearrange("p e (t m) -> p e t m", t=4),
-            w1w_b[:].bitcast(U16).rearrange("p e (m t) -> p e t m", t=4),
-        )
-        for e in range(FIRST_LOAD, E):
-            words_by_t[e] = last_words[:, e - FIRST_LOAD, :]
-        xg_late = held([P, 2 * WORD_PIECE], U32, "xg_late", "late")
-        for g in range(2):
-            unit_words.extend(gather(xg_late[:, g * WORD_PIECE : (g + 1) * WORD_PIECE], xw[:].bitcast(U32), (2 + g) * WORD_PIECE))
+        for e in range(TURNED + 1, E):
+            permute_words(e)
         shared_words = held([P, H], I32, "w1s_words_by_t")
         shared_plane = held([P, H], U8, "w1s_plane_by_t")
         nc.gpsimd.tensor_copy(shared_words[:].rearrange("p (t m) -> p t m", t=4), w1sw[:].rearrange("p (m t) -> p t m", t=4))
@@ -212,6 +202,11 @@ def tile_moe_shf_mlp_silu_kernel(
         acts = {}
         for u in range(2 * TURNED):
             acts[u] = first_turned(banks[first_ring[u % 5]], u, unit_words[u], unit_plane[u], u // 2)
+        xg_late = held([P, 2 * WORD_PIECE], U32, "xg_late", "early0")
+        for g in range(2):
+            unit_words.extend(gather(xg_late[:, g * WORD_PIECE : (g + 1) * WORD_PIECE], xw[:].bitcast(U32), (2 + g) * WORD_PIECE))
+        xgp_last = held([P, BYTE_PIECES[-1]], U8, "xgp_last", "early1")
+        unit_plane.extend(gather(xgp_last[:], xs[:].bitcast(U8), SLOTS - BYTE_PIECES[-1]))
         for e in range(TURNED):
             for a in range(2):
                 turn(banks[3 + e], a, acts[2 * e + a])
@@ -232,9 +227,9 @@ def tile_moe_shf_mlp_silu_kernel(
             if e < E - 1:
                 quantise(h_codes[e], h_plane[e], grouped[e], 0, C)
 
-        second(0, 0, 512, banks[5], nc.vector)
+        second(0, 0, 512, banks[7], nc.scalar)
         second(0, 512, 1024, banks[0], nc.scalar)
-        second(0, 1024, 1408, banks[3], nc.scalar)
+        second(0, 1024, 1408, banks[3], nc.vector)
         second(0, 1408, 1536, banks[4], nc.vector)
 
         blocks = T // P
@@ -286,41 +281,41 @@ def tile_moe_shf_mlp_silu_kernel(
 
         for r in range(TOP):
             fetch(0, r)
-        for b, bank in enumerate((2, 6, 7, 1)):
+        for b, bank in enumerate((7, 0, 3, 4)):
             first_direct(
                 banks[bank], hs_grouped[:, b * H : (b + 1) * H], xw[:, b * P : (b + 1) * P],
                 xs[:].bitcast(U8)[:, b * P : (b + 1) * P], shared_words[:].bitcast(FP8X4), shared_plane[:],
             )
         quantise(hs_codes, hs_plane, hs_grouped, 0, T)
-        second_tile(1, (5, 0, 3))
+        second_tile(1, (2, 6, 5))
         for r in range(TOP):
             fetch(1, r)
-        second_tile(2, (4, 2, 6))
+        second_tile(2, (1, 7, 0))
         for r in range(TOP):
             fetch(2, r)
-        flip(0, banks[7])
-        ys0 = shared_second(0, banks[1])
-        second_tile(3, (5, 0, 3))
+        flip(0, banks[3])
+        ys0 = shared_second(0, banks[4])
+        second_tile(3, (2, 6, 5))
         last = N // P - 1
         halves = ((0, T // 2), (T // 2, T))
         fetch(last, 0)
         for r in range(1, TOP):
             for lo, hi in halves:
                 fetch(last, r, lo, hi)
-        ys1 = shared_second(1, banks[4])
-        finish(0, ys0, banks[2])
-        flip(1, banks[6])
-        ys2 = shared_second(2, banks[7])
-        ys3 = shared_second(3, banks[1])
-        finish(1, ys1, banks[5])
-        back_banks = (banks[0], banks[3])
+        ys1 = shared_second(1, banks[1])
+        finish(0, ys0, banks[7])
+        flip(1, banks[0])
+        ys2 = shared_second(2, banks[3])
+        ys3 = shared_second(3, banks[4])
+        finish(1, ys1, banks[2])
+        back_banks = (banks[6], banks[5])
         for (lo, hi), bank in zip(halves, back_banks):
             turn_add(bank, ys3, True, False, lo, hi)
-        flip(2, banks[4])
-        flip_banks = (banks[2], banks[6])
+        flip(2, banks[1])
+        flip_banks = (banks[7], banks[0])
         for (lo, hi), bank in zip(halves, flip_banks):
             turn_add(bank, terms[last, 0], True, False, lo, hi)
-        finish(2, ys2, banks[7])
+        finish(2, ys2, banks[3])
         for (lo, hi), bank in zip(halves, flip_banks):
             turn_add(bank, terms[last, 1], False, True, lo, hi)
             nc.scalar.copy(flipped[last][:, lo:hi], bank[:, 0 : hi - lo])

@@ -55,14 +55,12 @@ def tile_moe_shf_mlp_silu_kernel(
         w2sp = held([P, N // 4], I32, "w2sp")
         gate_sb = [held([P, T], F32, "gate_sb%d" % r) for r in range(TOP)]
         ident = held([P, P], F32, "ident")
-        warm = held([P, 8], F32, "warm")
 
         def w1w(e):
             return w1w_a[:, e, :] if e < FIRST_LOAD else w1w_b[:, e - FIRST_LOAD, :]
 
         nc.vector.memset(w1p[:], 0)
         nc.vector.memset(w1sp[:], 0)
-        nc.gpsimd.memset(warm[:], 0.0)
         make_identity(nc, ident[:])
         nc.gpsimd.memset(w2p[:], 0)
         nc.gpsimd.memset(w2sp[:], 0)
@@ -89,13 +87,12 @@ def tile_moe_shf_mlp_silu_kernel(
         load_words(nc.sync, xw[:], x_words)
         for q in range(4):
             load_token_rows(nc.sync if q < 1 else nc.scalar, q)
-        nc.scalar.activation(warm[:], warm[:], SILU)
         load_experts(nc.sync, w1w_a[:], w1_words, 0, FIRST_LOAD)
         for q in range(4):
-            load_expert_rows(nc.sync if q < 3 else nc.scalar, w1p, w1_scales, q)
+            load_expert_rows(nc.sync if q < 2 else nc.scalar, w1p, w1_scales, q)
         load_experts(nc.sync, w1w_b[:], w1_words, FIRST_LOAD, E)
         for q in range(4):
-            load_rows(nc.scalar, w1sp, w1s_scales, q)
+            load_rows(nc.scalar if q < 2 else nc.sync, w1sp, w1s_scales, q)
         load_words(nc.sync, w1sw[:], w1s_words)
         load_experts(nc.sync, w2w[:], w2_words, 0, E)
         for q in range(4):
@@ -124,9 +121,9 @@ def tile_moe_shf_mlp_silu_kernel(
         words_by_t = {}
         planes_by_t = held([P, direct, H], U8, "planes_by_t")
 
-        def permute_words(e):
+        def permute_words(e, engine=nc.gpsimd):
             words = held([P, H], U16, "w1_words_by_t%d" % e)
-            nc.gpsimd.tensor_copy(
+            engine.tensor_copy(
                 words[:].rearrange("p (t m) -> p t m", t=4), w1w(e).bitcast(U16).rearrange("p (m t) -> p t m", t=4),
             )
             words_by_t[e] = words[:].bitcast(U8)
@@ -136,7 +133,7 @@ def tile_moe_shf_mlp_silu_kernel(
             planes_by_t[:].rearrange("p e (t m) -> p e t m", t=4),
             w1p[:, TURNED:E, :].bitcast(U8).rearrange("p e (m t) -> p e t m", t=4),
         )
-        for e in range(TURNED + 1, E):
+        for e in range(TURNED + 1, E - 1):
             permute_words(e)
         shared_words = held([P, H], I32, "w1s_words_by_t")
         shared_plane = held([P, H], U8, "w1s_plane_by_t")
@@ -205,6 +202,7 @@ def tile_moe_shf_mlp_silu_kernel(
         xg_late = held([P, 2 * WORD_PIECE], U32, "xg_late", "early0")
         for g in range(2):
             unit_words.extend(gather(xg_late[:, g * WORD_PIECE : (g + 1) * WORD_PIECE], xw[:].bitcast(U32), (2 + g) * WORD_PIECE))
+        permute_words(E - 1, nc.vector)
         xgp_last = held([P, BYTE_PIECES[-1]], U8, "xgp_last", "early1")
         unit_plane.extend(gather(xgp_last[:], xs[:].bitcast(U8), SLOTS - BYTE_PIECES[-1]))
         for e in range(TURNED):

@@ -20,8 +20,9 @@ SILU = mybir.ActivationFunctionType.Silu
 MULT = mybir.AluOpType.mult
 ADD = mybir.AluOpType.add
 
-BYTE_PIECES = (128, 128, 256, 256, 384, 384)
-WORD_PIECE = 384
+BYTE_PIECES = (128, 256, 384, 384, 384)
+WORD_PIECE = 768
+WINDOW = 1024
 TURNED = 3
 FIRST_LOAD = 4
 
@@ -42,7 +43,8 @@ def tile_moe_shf_mlp_silu_kernel(
 
         offs_sb = keep.tile([P, SLOTS // 16], U16, name="offs_sb")
         pos_sb = [keep.tile([P, T // 16], U16, name="pos_sb%d" % r) for r in range(TOP)]
-        xw = held([P, T], I32, "xw")
+        xw_window = held([P, WINDOW], I32, "xw_window")
+        xw = xw_window[:, 0:T]
         xs = held([P, T // 4], I32, "xs")
         w1w_a = held([P, FIRST_LOAD, 2 * H], U8, "w1w_a")
         w1w_b = held([P, E - FIRST_LOAD, 2 * H], U8, "w1w_b")
@@ -53,7 +55,7 @@ def tile_moe_shf_mlp_silu_kernel(
         w2sw = held([P, N], I32, "w2sw")
         w1sp = held([P, H // 4], I32, "w1sp")
         w2sp = held([P, N // 4], I32, "w2sp")
-        gate_sb = [held([P, T], F32, "gate_sb%d" % r) for r in range(TOP)]
+        gate_sb = [held([P, T], F32, "gate_sb%d" % r, "gate%d" % r) for r in range(TOP)]
         ident = held([P, P], F32, "ident")
 
         def w1w(e):
@@ -61,6 +63,7 @@ def tile_moe_shf_mlp_silu_kernel(
 
         nc.vector.memset(w1p[:], 0)
         nc.vector.memset(w1sp[:], 0)
+        nc.vector.memset(xw_window[:, T:WINDOW], 0)
         make_identity(nc, ident[:])
         nc.gpsimd.memset(w2p[:], 0)
         nc.gpsimd.memset(w2sp[:], 0)
@@ -83,8 +86,8 @@ def tile_moe_shf_mlp_silu_kernel(
             rows = x_scales[0, 4 * q : 4 * q + 4, :].bitcast(I32)
             queue.dma_start(xs[32 * q : 32 * q + 32, :], rows.unsqueeze(0).to_broadcast([8, 4, T // 4]))
 
+        load_words(nc.sync, xw, x_words)
         nc.sync.dma_start(offs_sb[:], offs)
-        load_words(nc.sync, xw[:], x_words)
         for q in range(4):
             load_token_rows(nc.sync if q < 1 else nc.scalar, q)
         load_experts(nc.sync, w1w_a[:], w1_words, 0, FIRST_LOAD)
@@ -110,11 +113,10 @@ def tile_moe_shf_mlp_silu_kernel(
             return [picked[:, a : a + P] for a in range(0, cols, P)]
 
         unit_words, unit_plane = [], []
-        for g in range(2):
-            xg = held([P, WORD_PIECE], U32, "xg%d" % g, "early%d" % g)
-            unit_words.extend(gather(xg[:], xw[:].bitcast(U32), g * WORD_PIECE))
+        xg = held([P, WORD_PIECE], U32, "xg")
+        unit_words.extend(gather(xg[:], xw_window[:].bitcast(U32), 0))
         for g, cols in enumerate(BYTE_PIECES[:-1]):
-            xgp = held([P, cols], U8, "xgp%d" % g)
+            xgp = held([P, cols], U8, "xgp%d" % g, "early%d" % g)
             unit_plane.extend(gather(xgp[:], xs[:].bitcast(U8), sum(BYTE_PIECES[:g])))
 
         direct = E - TURNED
@@ -199,31 +201,37 @@ def tile_moe_shf_mlp_silu_kernel(
         acts = {}
         for u in range(2 * TURNED):
             acts[u] = first_turned(banks[first_ring[u % 5]], u, unit_words[u], unit_plane[u], u // 2)
-        xg_late = held([P, 2 * WORD_PIECE], U32, "xg_late", "early0")
-        for g in range(2):
-            unit_words.extend(gather(xg_late[:, g * WORD_PIECE : (g + 1) * WORD_PIECE], xw[:].bitcast(U32), (2 + g) * WORD_PIECE))
+        xg_late = held([P, WORD_PIECE], U32, "xg_late", "early0")
+        unit_words.extend(gather(xg_late[:], xw_window[:].bitcast(U32), WORD_PIECE))
         permute_words(E - 1, nc.vector)
-        xgp_last = held([P, BYTE_PIECES[-1]], U8, "xgp_last", "early1")
+        xgp_last = held([P, BYTE_PIECES[-1]], U8, "xgp_last", "early2")
         unit_plane.extend(gather(xgp_last[:], xs[:].bitcast(U8), SLOTS - BYTE_PIECES[-1]))
-        for e in range(TURNED):
+
+        def turn_expert(e):
             for a in range(2):
                 turn(banks[3 + e], a, acts[2 * e + a])
             src = banks[3 + e][:].rearrange("p (a u s) -> p a s u", u=2, s=P)
             dst = grouped[e][:].bitcast(F32).rearrange("p (a s u) -> p a s u", u=2, s=P)
             copy_out(nc.scalar if e == 0 else nc.vector, dst, src)
-        for e in range(TURNED):
+
+        def direct_unit(u, bank):
+            e, a = divmod(u, 2)
+            first_direct(
+                bank, grouped[e][:, a * H : (a + 1) * H], unit_words[u], unit_plane[u],
+                words_by_t[e].bitcast(FP4X4), planes_by_t[:, e - TURNED, :],
+            )
+
+        for e in range(TURNED - 1):
+            turn_expert(e)
+        direct_unit(2 * TURNED, banks[3 + TURNED - 1])
+        direct_unit(2 * TURNED + 1, banks[first_ring[(2 * TURNED + 1) % 5]])
+        turn_expert(TURNED - 1)
+        for u in range(2 * TURNED + 2, 2 * E):
+            direct_unit(u, banks[first_ring[u % 5]])
+        for e in range(E - 1):
             quantise(h_codes[e], h_plane[e], grouped[e], 0, C)
-        for e in range(TURNED, E):
-            for a in range(2):
-                u = 2 * e + a
-                first_direct(
-                    banks[first_ring[u % 5]], grouped[e][:, a * H : (a + 1) * H], unit_words[u], unit_plane[u],
-                    words_by_t[e].bitcast(FP4X4), planes_by_t[:, e - TURNED, :],
-                )
-                if e == E - 1:
-                    quantise(h_codes[e], h_plane[e], grouped[e], a * P, (a + 1) * P)
-            if e < E - 1:
-                quantise(h_codes[e], h_plane[e], grouped[e], 0, C)
+        for a in range(2):
+            quantise(h_codes[E - 1], h_plane[E - 1], grouped[E - 1], a * P, (a + 1) * P)
 
         second(0, 0, 512, banks[7], nc.scalar)
         second(0, 512, 1024, banks[0], nc.scalar)
@@ -231,11 +239,13 @@ def tile_moe_shf_mlp_silu_kernel(
         second(0, 1408, 1536, banks[4], nc.vector)
 
         blocks = T // P
-        terms = {(j, r): held([P, T], F32, "term%d_%d" % (j, r)) for j in range(N // P) for r in range(TOP)}
+        terms = {}
 
-        def fetch(j, r, lo=0, hi=T):
+        def fetch(j, r, lo=0, hi=T, tag=""):
+            term = held([P, hi - lo], F32, "term%d_%d_%d" % (j, r, lo), tag)
             picks = pos_sb[r][:, lo // 16 : hi // 16]
-            nc.vector.tensor_tensor(terms[j, r][:, lo:hi], y_sb[j][:].indirect(picks), gate_sb[r][:, lo:hi], MULT)
+            nc.vector.tensor_tensor(term[:], y_sb[j][:].indirect(picks), gate_sb[r][:, lo:hi], MULT)
+            terms[j, r, lo] = term
 
         def turn_add(bank, source, opens, closes, lo=0, hi=T):
             for at in range(lo, hi, P):
@@ -249,7 +259,7 @@ def tile_moe_shf_mlp_silu_kernel(
 
         def flip(j, bank):
             for r in range(TOP):
-                turn_add(bank, terms[j, r], r == 0, r == TOP - 1)
+                turn_add(bank, terms[j, r, 0], r == 0, r == TOP - 1)
             nc.scalar.copy(flipped[j][:], bank[:])
 
         hs_grouped = held([P, 4 * T], BF16, "hs_grouped")
@@ -289,36 +299,44 @@ def tile_moe_shf_mlp_silu_kernel(
         for r in range(TOP):
             fetch(1, r)
         second_tile(2, (1, 7, 0))
-        for r in range(TOP):
+        for r in range(TOP - 1):
             fetch(2, r)
         flip(0, banks[3])
         ys0 = shared_second(0, banks[4])
         second_tile(3, (2, 6, 5))
-        last = N // P - 1
-        halves = ((0, T // 2), (T // 2, T))
-        fetch(last, 0)
-        for r in range(1, TOP):
-            for lo, hi in halves:
-                fetch(last, r, lo, hi)
+        for r in range(TOP - 1):
+            fetch(3, r)
         ys1 = shared_second(1, banks[1])
         finish(0, ys0, banks[7])
         flip(1, banks[0])
-        ys2 = shared_second(2, banks[3])
-        ys3 = shared_second(3, banks[4])
+        ys = {2: shared_second(2, banks[3]), 3: shared_second(3, banks[4])}
         finish(1, ys1, banks[2])
-        back_banks = (banks[6], banks[5])
-        for (lo, hi), bank in zip(halves, back_banks):
-            turn_add(bank, ys3, True, False, lo, hi)
-        flip(2, banks[1])
-        flip_banks = (banks[7], banks[0])
-        for (lo, hi), bank in zip(halves, flip_banks):
-            turn_add(bank, terms[last, 0], True, False, lo, hi)
-        finish(2, ys2, banks[3])
-        for (lo, hi), bank in zip(halves, flip_banks):
-            turn_add(bank, terms[last, 1], False, True, lo, hi)
-            nc.scalar.copy(flipped[last][:, lo:hi], bank[:, 0 : hi - lo])
-        for (lo, hi), bank in zip(halves, back_banks):
-            turn_add(bank, flipped[last], False, True, lo, hi)
-        for (lo, hi), bank in zip(halves, back_banks):
-            nc.vector.tensor_tensor(res[last][:, lo:hi], bank[:, 0 : hi - lo], terms[last, TOP - 1][:, lo:hi], ADD)
-            nc.sync.dma_start(out[last * P : (last + 1) * P, lo:hi], res[last][:, lo:hi])
+
+        half = T // 2
+        flip_bank = {(2, 0): banks[1], (2, half): banks[7], (3, 0): banks[0], (3, half): banks[2]}
+        back_bank = {(2, 0): banks[3], (2, half): banks[6], (3, 0): banks[4], (3, half): banks[5]}
+        for j in (2, 3):
+            for lo in (half, 0):
+                turn_add(back_bank[j, lo], ys[j], True, False, lo, lo + half)
+
+        def flip_back(j, lo):
+            nc.scalar.copy(flipped[j][:, lo : lo + half], flip_bank[j, lo][:, 0:half])
+            turn_add(back_bank[j, lo], flipped[j], False, True, lo, lo + half)
+
+        for j in (2, 3):
+            for r in range(TOP - 1):
+                for lo in (half, 0):
+                    turn_add(flip_bank[j, lo], terms[j, r, 0], r == 0, lo == half and r == TOP - 2, lo, lo + half)
+            flip_back(j, half)
+        for j, tag in ((2, "gate0"), (3, "")):
+            fetch(j, TOP - 1, 0, half, tag)
+        fetch(2, TOP - 1, half, T, "gate1")
+        for j in (2, 3):
+            turn_add(flip_bank[j, 0], terms[j, TOP - 1, 0], False, True, 0, half)
+            flip_back(j, 0)
+            nc.scalar.copy(res[j][:, 0:half], back_bank[j, 0][:, 0:half])
+            nc.sync.dma_start(out[j * P : (j + 1) * P, 0:half], res[j][:, 0:half])
+        fetch(3, TOP - 1, half, T)
+        for j in (2, 3):
+            nc.vector.tensor_tensor(res[j][:, half:T], back_bank[j, half][:, 0:half], terms[j, TOP - 1, half][:], ADD)
+            nc.sync.dma_start(out[j * P : (j + 1) * P, half:T], res[j][:, half:T])

@@ -24,7 +24,6 @@ BYTE_PIECES = (128, 256, 384, 384, 384)
 WORD_PIECE = 768
 WINDOW = 1024
 TURNED = 3
-FIRST_LOAD = 4
 
 
 def tile_moe_shf_mlp_silu_kernel(
@@ -46,8 +45,7 @@ def tile_moe_shf_mlp_silu_kernel(
         xw_window = held([P, WINDOW], I32, "xw_window")
         xw = xw_window[:, 0:T]
         xs = held([P, T // 4], I32, "xs")
-        w1w_a = held([P, FIRST_LOAD, 2 * H], U8, "w1w_a")
-        w1w_b = held([P, E - FIRST_LOAD, 2 * H], U8, "w1w_b")
+        w1w_pair = [held([P, 2, 2 * H], U8, "w1w_pair%d" % g) for g in range(E // 2)]
         w2w = held([P, E, 2 * N], U8, "w2w")
         w1p = held([P, E, H // 4], I32, "w1p")
         w2p = held([P, E, N // 4], I32, "w2p")
@@ -59,8 +57,9 @@ def tile_moe_shf_mlp_silu_kernel(
         ident = held([P, P], F32, "ident")
 
         def w1w(e):
-            return w1w_a[:, e, :] if e < FIRST_LOAD else w1w_b[:, e - FIRST_LOAD, :]
+            return w1w_pair[e // 2][:, e % 2, :]
 
+        nc.gpsimd.memset(xs[:], 0)
         nc.vector.memset(w1p[:], 0)
         nc.vector.memset(w1sp[:], 0)
         nc.vector.memset(xw_window[:, T:WINDOW], 0)
@@ -82,20 +81,17 @@ def tile_moe_shf_mlp_silu_kernel(
             rows = dram[:, 0, 4 * q : 4 * q + 4, :].rearrange("e r n -> r e n")
             queue.dma_start(plane[32 * q : 32 * q + 4, :, :], rows.bitcast(I32))
 
-        def load_token_rows(queue, q):
-            rows = x_scales[0, 4 * q : 4 * q + 4, :].bitcast(I32)
-            queue.dma_start(xs[32 * q : 32 * q + 32, :], rows.unsqueeze(0).to_broadcast([8, 4, T // 4]))
-
         load_words(nc.sync, xw, x_words)
         nc.sync.dma_start(offs_sb[:], offs)
         for q in range(4):
-            load_token_rows(nc.sync if q < 1 else nc.scalar, q)
-        load_experts(nc.sync, w1w_a[:], w1_words, 0, FIRST_LOAD)
+            load_rows(nc.scalar, xs, x_scales, q)
+        load_experts(nc.sync, w1w_pair[0][:], w1_words, 0, 2)
         for q in range(4):
             load_expert_rows(nc.sync if q < 2 else nc.scalar, w1p, w1_scales, q)
-        load_experts(nc.sync, w1w_b[:], w1_words, FIRST_LOAD, E)
+        for g in range(1, E // 2):
+            load_experts(nc.sync, w1w_pair[g][:], w1_words, 2 * g, 2 * g + 2)
         for q in range(4):
-            load_rows(nc.scalar if q < 2 else nc.sync, w1sp, w1s_scales, q)
+            load_rows(nc.sync, w1sp, w1s_scales, q)
         load_words(nc.sync, w1sw[:], w1s_words)
         load_experts(nc.sync, w2w[:], w2_words, 0, E)
         for q in range(4):

@@ -24,6 +24,7 @@ BYTE_PIECES = (128, 256, 384, 384, 384)
 WORD_PIECE = 768
 WINDOW = 1024
 TURNED = 3
+W1_LOADS = ((0, 1), (1, 3), (3, 6))
 
 
 def tile_moe_shf_mlp_silu_kernel(
@@ -45,7 +46,7 @@ def tile_moe_shf_mlp_silu_kernel(
         xw_window = held([P, WINDOW], I32, "xw_window")
         xw = xw_window[:, 0:T]
         xs = held([P, T // 4], I32, "xs")
-        w1w_pair = [held([P, 2, 2 * H], U8, "w1w_pair%d" % g) for g in range(E // 2)]
+        w1w_load = [held([P, hi - lo, 2 * H], U8, "w1w_load%d" % lo) for lo, hi in W1_LOADS]
         w2w = held([P, E, 2 * N], U8, "w2w")
         w1p = held([P, E, H // 4], I32, "w1p")
         w2p = held([P, E, N // 4], I32, "w2p")
@@ -57,7 +58,8 @@ def tile_moe_shf_mlp_silu_kernel(
         ident = held([P, P], F32, "ident")
 
         def w1w(e):
-            return w1w_pair[e // 2][:, e % 2, :]
+            g = max(g for g, (lo, hi) in enumerate(W1_LOADS) if lo <= e)
+            return w1w_load[g][:, e - W1_LOADS[g][0], :]
 
         nc.gpsimd.memset(xs[:], 0)
         nc.vector.memset(w1p[:], 0)
@@ -85,13 +87,14 @@ def tile_moe_shf_mlp_silu_kernel(
         nc.sync.dma_start(offs_sb[:], offs)
         for q in range(4):
             load_rows(nc.scalar, xs, x_scales, q)
-        load_experts(nc.sync, w1w_pair[0][:], w1_words, 0, 2)
+        load_experts(nc.sync, w1w_load[0][:], w1_words, *W1_LOADS[0])
         for q in range(4):
             load_expert_rows(nc.sync if q < 2 else nc.scalar, w1p, w1_scales, q)
-        for g in range(1, E // 2):
-            load_experts(nc.sync, w1w_pair[g][:], w1_words, 2 * g, 2 * g + 2)
+        load_experts(nc.sync, w1w_load[1][:], w1_words, *W1_LOADS[1])
         for q in range(4):
             load_rows(nc.sync, w1sp, w1s_scales, q)
+            if q == 1:
+                load_experts(nc.sync, w1w_load[2][:], w1_words, *W1_LOADS[2])
         load_words(nc.sync, w1sw[:], w1s_words)
         load_experts(nc.sync, w2w[:], w2_words, 0, E)
         for q in range(4):
@@ -126,12 +129,11 @@ def tile_moe_shf_mlp_silu_kernel(
             )
             words_by_t[e] = words[:].bitcast(U8)
 
-        permute_words(TURNED)
         nc.gpsimd.tensor_copy(
             planes_by_t[:].rearrange("p e (t m) -> p e t m", t=4),
             w1p[:, TURNED:E, :].bitcast(U8).rearrange("p e (m t) -> p e t m", t=4),
         )
-        for e in range(TURNED + 1, E - 1):
+        for e in range(TURNED, E):
             permute_words(e)
         shared_words = held([P, H], I32, "w1s_words_by_t")
         shared_plane = held([P, H], U8, "w1s_plane_by_t")
@@ -199,7 +201,6 @@ def tile_moe_shf_mlp_silu_kernel(
             acts[u] = first_turned(banks[first_ring[u % 5]], u, unit_words[u], unit_plane[u], u // 2)
         xg_late = held([P, WORD_PIECE], U32, "xg_late", "early0")
         unit_words.extend(gather(xg_late[:], xw_window[:].bitcast(U32), WORD_PIECE))
-        permute_words(E - 1, nc.vector)
         xgp_last = held([P, BYTE_PIECES[-1]], U8, "xgp_last", "early2")
         unit_plane.extend(gather(xgp_last[:], xs[:].bitcast(U8), SLOTS - BYTE_PIECES[-1]))
 

@@ -296,8 +296,10 @@ def tile_moe_shf_mlp_silu_kernel(
         for r in range(TOP):
             fetch(1, r)
         second_tile(2, (1, 7, 0))
+        half = T // 2
         for r in range(TOP - 1):
             fetch(2, r)
+        fetch(2, TOP - 1, 0, half)
         flip(0, banks[3])
         ys0 = shared_second(0, banks[4])
         second_tile(3, (2, 6, 5))
@@ -309,7 +311,6 @@ def tile_moe_shf_mlp_silu_kernel(
         ys = {2: shared_second(2, banks[3]), 3: shared_second(3, banks[4])}
         finish(1, ys1, banks[2])
 
-        half = T // 2
         flip_bank = {(2, 0): banks[1], (2, half): banks[7], (3, 0): banks[0], (3, half): banks[2]}
         back_bank = {(2, 0): banks[3], (2, half): banks[6], (3, 0): banks[4], (3, half): banks[5]}
         for j in (2, 3):
@@ -324,11 +325,10 @@ def tile_moe_shf_mlp_silu_kernel(
             for r in range(TOP - 1):
                 for lo in (half, 0):
                     turn_add(flip_bank[j, lo], terms[j, r, 0], r == 0, lo == half and r == TOP - 2, lo, lo + half)
+            if j == 3:
+                fetch(3, TOP - 1, 0, half)
+                fetch(2, TOP - 1, half, T, "gate1")
             flip_back(j, half)
-        for j, tag in ((2, "gate0"), (3, "")):
-            fetch(j, TOP - 1, 0, half, tag)
-        fetch(2, TOP - 1, half, T, "gate1")
-        for j in (2, 3):
             turn_add(flip_bank[j, 0], terms[j, TOP - 1, 0], False, True, 0, half)
             flip_back(j, 0)
             nc.scalar.copy(res[j][:, 0:half], back_bank[j, 0][:, 0:half])

@@ -6,6 +6,7 @@ from concourse.masks import make_identity
 K, T, E, C, H, N, TOP = 512, 512, 6, 256, 512, 512, 3
 SLOTS = E * C
 P = 128
+BANK = 512
 FLOPS = 2 * (SLOTS + T) * (K * H + H * N)
 
 F32 = mybir.dt.float32
@@ -20,11 +21,11 @@ SILU = mybir.ActivationFunctionType.Silu
 MULT = mybir.AluOpType.mult
 ADD = mybir.AluOpType.add
 
-BYTE_PIECES = (128, 256, 384, 384, 384)
-WORD_PIECE = 768
-WINDOW = 1024
 TURNED = 3
-W1_LOADS = ((0, 1), (1, 3), (3, 6))
+BYTE_PIECES = (128, 256, 384, 384, 384)
+WORD_PIECE = TURNED * C
+WINDOW = 1024
+W1_LOADS = ((0, 1), (1, TURNED), (TURNED, E))
 
 
 def tile_moe_shf_mlp_silu_kernel(
@@ -39,7 +40,7 @@ def tile_moe_shf_mlp_silu_kernel(
         def held(shape, dtype, name, tag=""):
             return keep.tile(shape, dtype, name=name, tag=tag, align_bytes=64)
 
-        banks = [psum.tile([P, 512], F32, name="bank%d" % b) for b in range(8)]
+        banks = [psum.tile([P, BANK], F32, name="bank%d" % b) for b in range(8)]
 
         offs_sb = keep.tile([P, SLOTS // 16], U16, name="offs_sb")
         pos_sb = [keep.tile([P, T // 16], U16, name="pos_sb%d" % r) for r in range(TOP)]
@@ -69,12 +70,12 @@ def tile_moe_shf_mlp_silu_kernel(
         nc.gpsimd.memset(w2p[:], 0)
         nc.gpsimd.memset(w2sp[:], 0)
 
-        def load_words(queue, tile_ap, dram):
-            queue.dma_start(tile_ap, dram[0].rearrange("p n d -> p (n d)").bitcast(I32))
+        def load_words(tile_ap, dram):
+            nc.sync.dma_start(tile_ap, dram[0].rearrange("p n d -> p (n d)").bitcast(I32))
 
-        def load_experts(queue, tile_ap, dram, lo, hi):
+        def load_experts(tile_ap, dram, lo, hi):
             rows = dram[lo:hi, 0].rearrange("e p n -> p e n")
-            queue.dma_start(tile_ap.bitcast(I32), rows.bitcast(I32))
+            nc.sync.dma_start(tile_ap.bitcast(I32), rows.bitcast(I32))
 
         def load_rows(queue, plane, dram, q):
             queue.dma_start(plane[32 * q : 32 * q + 4, :], dram[0, 4 * q : 4 * q + 4, :].bitcast(I32))
@@ -83,26 +84,27 @@ def tile_moe_shf_mlp_silu_kernel(
             rows = dram[:, 0, 4 * q : 4 * q + 4, :].rearrange("e r n -> r e n")
             queue.dma_start(plane[32 * q : 32 * q + 4, :, :], rows.bitcast(I32))
 
-        load_words(nc.sync, xw, x_words)
+        load_words(xw, x_words)
         nc.sync.dma_start(offs_sb[:], offs)
         for q in range(4):
             load_rows(nc.scalar, xs, x_scales, q)
-        load_experts(nc.sync, w1w_load[0][:], w1_words, *W1_LOADS[0])
+        load_experts(w1w_load[0][:], w1_words, *W1_LOADS[0])
         for q in range(4):
             load_expert_rows(nc.sync if q < 2 else nc.scalar, w1p, w1_scales, q)
-        load_experts(nc.sync, w1w_load[1][:], w1_words, *W1_LOADS[1])
-        for q in range(4):
+        load_experts(w1w_load[1][:], w1_words, *W1_LOADS[1])
+        for q in range(2):
             load_rows(nc.sync, w1sp, w1s_scales, q)
-            if q == 1:
-                load_experts(nc.sync, w1w_load[2][:], w1_words, *W1_LOADS[2])
-        load_words(nc.sync, w1sw[:], w1s_words)
-        load_experts(nc.sync, w2w[:], w2_words, 0, E)
+        load_experts(w1w_load[2][:], w1_words, *W1_LOADS[2])
+        for q in range(2, 4):
+            load_rows(nc.sync, w1sp, w1s_scales, q)
+        load_words(w1sw[:], w1s_words)
+        load_experts(w2w[:], w2_words, 0, E)
         for q in range(4):
             load_expert_rows(nc.sync, w2p, w2_scales, q)
         for r, pos in enumerate((pos1, pos2, pos3)):
             nc.sync.dma_start(pos_sb[r][:], pos)
             nc.sync.dma_start(gate_sb[r][:], gate[r])
-        load_words(nc.sync, w2sw[:], w2s_words)
+        load_words(w2sw[:], w2s_words)
         for q in range(4):
             load_rows(nc.sync, w2sp, w2s_scales, q)
 
@@ -118,27 +120,26 @@ def tile_moe_shf_mlp_silu_kernel(
             xgp = held([P, cols], U8, "xgp%d" % g, "early%d" % g)
             unit_plane.extend(gather(xgp[:], xs[:].bitcast(U8), sum(BYTE_PIECES[:g])))
 
-        direct = E - TURNED
         words_by_t = {}
-        planes_by_t = held([P, direct, H], U8, "planes_by_t")
-
-        def permute_words(e, engine=nc.gpsimd):
-            words = held([P, H], U16, "w1_words_by_t%d" % e)
-            engine.tensor_copy(
-                words[:].rearrange("p (t m) -> p t m", t=4), w1w(e).bitcast(U16).rearrange("p (m t) -> p t m", t=4),
-            )
-            words_by_t[e] = words[:].bitcast(U8)
-
+        planes_by_t = held([P, E - TURNED, H], U8, "planes_by_t")
         nc.gpsimd.tensor_copy(
             planes_by_t[:].rearrange("p e (t m) -> p e t m", t=4),
             w1p[:, TURNED:E, :].bitcast(U8).rearrange("p e (m t) -> p e t m", t=4),
         )
         for e in range(TURNED, E):
-            permute_words(e)
+            words = held([P, H], U16, "w1_words_by_t%d" % e)
+            nc.gpsimd.tensor_copy(
+                words[:].rearrange("p (t m) -> p t m", t=4), w1w(e).bitcast(U16).rearrange("p (m t) -> p t m", t=4),
+            )
+            words_by_t[e] = words[:].bitcast(U8)
         shared_words = held([P, H], I32, "w1s_words_by_t")
         shared_plane = held([P, H], U8, "w1s_plane_by_t")
-        nc.gpsimd.tensor_copy(shared_words[:].rearrange("p (t m) -> p t m", t=4), w1sw[:].rearrange("p (m t) -> p t m", t=4))
-        nc.gpsimd.tensor_copy(shared_plane[:].rearrange("p (t m) -> p t m", t=4), w1sp[:].bitcast(U8).rearrange("p (m t) -> p t m", t=4))
+        nc.gpsimd.tensor_copy(
+            shared_words[:].rearrange("p (t m) -> p t m", t=4), w1sw[:].rearrange("p (m t) -> p t m", t=4),
+        )
+        nc.gpsimd.tensor_copy(
+            shared_plane[:].rearrange("p (t m) -> p t m", t=4), w1sp[:].bitcast(U8).rearrange("p (m t) -> p t m", t=4),
+        )
 
         def copy_out(engine, dst, src):
             if engine is nc.vector:
@@ -146,40 +147,35 @@ def tile_moe_shf_mlp_silu_kernel(
             else:
                 nc.scalar.copy(dst, src)
 
-        def first_turned(acc, u, x_codes, x_plane, e):
+        def first_turned(u, bank):
+            e = u // 2
             nc.tensor.matmul_mx(
-                out=acc[:], lhsT=x_codes.bitcast(FP8X4), lhsT_scale=x_plane,
+                out=bank[:], lhsT=unit_words[u].bitcast(FP8X4), lhsT_scale=unit_plane[u],
                 rhs=w1w(e).bitcast(FP4X4), rhs_scale=w1p[:, e, :].bitcast(U8), start=True, stop=True,
             )
-            act = held([P, H], BF16, "act_%d" % u)
+            act = held([P, H], BF16, "act_%d" % u, "act_%d" % u)
             nc.scalar.activation(
-                act[:].rearrange("s (u p e) -> s u p e", u=2, e=2),
-                acc[:].rearrange("s (p u e) -> s u p e", u=2, e=2), SILU,
+                act[:].rearrange("s (w p d) -> s w p d", w=2, d=2),
+                bank[:].rearrange("s (p w d) -> s w p d", w=2, d=2), SILU,
             )
             return act
 
-        def turn(turned, a, act):
-            words = act[:].bitcast(F32)
-            for u in range(2):
-                col = (2 * a + u) * P
-                nc.tensor.transpose(turned[:, col : col + P], words[:, u * P : (u + 1) * P], ident[:])
-
-        def first_direct(acc, dst, x_codes, x_plane, words, plane):
+        def first_direct(bank, dst, x_codes, x_plane, words, plane):
             for t in range(4):
                 nc.tensor.matmul_mx(
-                    out=acc[:, t * P : (t + 1) * P], lhsT=words[:, t * P : (t + 1) * P],
+                    out=bank[:, t * P : (t + 1) * P], lhsT=words[:, t * P : (t + 1) * P],
                     lhsT_scale=plane[:, t * P : (t + 1) * P], rhs=x_codes.bitcast(FP8X4),
                     rhs_scale=x_plane, start=True, stop=True,
                 )
             nc.scalar.activation(
-                dst.rearrange("p (s t) -> p s t", t=4), acc[:].rearrange("p (t s) -> p s t", t=4), SILU,
+                dst.rearrange("p (s t) -> p s t", t=4), bank[:].rearrange("p (t s) -> p s t", t=4), SILU,
             )
 
-        def quantise(codes, plane, grouped, lo, hi):
-            nc.vector.quantize_mx(out=codes[:, lo:hi].bitcast(FP8X4), scales=plane[:, lo:hi], in_=grouped[:, 4 * lo : 4 * hi])
+        def quantise(codes, plane, values, lo, hi):
+            nc.vector.quantize_mx(out=codes[:, lo:hi].bitcast(FP8X4), scales=plane[:, lo:hi], in_=values[:, 4 * lo : 4 * hi])
 
         y_sb = [held([P, SLOTS], F32, "y_sb%d" % j) for j in range(N // P)]
-        h_codes = [held([P, C], U32, "h_codes%d" % e) for e in range(E)]
+        h_codes = {}
         h_plane = [held([P, C], U8, "h_plane%d" % e) for e in range(E)]
 
         def second(j, lo, hi, bank, engine):
@@ -195,10 +191,9 @@ def tile_moe_shf_mlp_silu_kernel(
             copy_out(engine, y_sb[j][:, lo:hi], bank[:, 0 : hi - lo])
 
         grouped = [held([P, 4 * C], BF16, "grouped%d" % e) for e in range(E)]
-        first_ring = (0, 1, 2, 6, 7)
-        acts = {}
-        for u in range(2 * TURNED):
-            acts[u] = first_turned(banks[first_ring[u % 5]], u, unit_words[u], unit_plane[u], u // 2)
+        ring = [banks[b] for b in (0, 1, 2, 6, 7)]
+        turn_bank = banks[3 : 3 + TURNED]
+        acts = [first_turned(u, ring[u % len(ring)]) for u in range(2 * TURNED)]
         xg_late = held([P, WORD_PIECE], U32, "xg_late", "early0")
         unit_words.extend(gather(xg_late[:], xw_window[:].bitcast(U32), WORD_PIECE))
         xgp_last = held([P, BYTE_PIECES[-1]], U8, "xgp_last", "early2")
@@ -206,9 +201,12 @@ def tile_moe_shf_mlp_silu_kernel(
 
         def turn_expert(e):
             for a in range(2):
-                turn(banks[3 + e], a, acts[2 * e + a])
-            src = banks[3 + e][:].rearrange("p (a u s) -> p a s u", u=2, s=P)
-            dst = grouped[e][:].bitcast(F32).rearrange("p (a s u) -> p a s u", u=2, s=P)
+                pairs = acts[2 * e + a][:].bitcast(F32)
+                for w in range(2):
+                    col = (2 * a + w) * P
+                    nc.tensor.transpose(turn_bank[e][:, col : col + P], pairs[:, w * P : (w + 1) * P], ident[:])
+            src = turn_bank[e][:].rearrange("p (a w s) -> p a s w", w=2, s=P)
+            dst = grouped[e][:].bitcast(F32).rearrange("p (a s w) -> p a s w", w=2, s=P)
             copy_out(nc.scalar if e == 0 else nc.vector, dst, src)
 
         def direct_unit(u, bank):
@@ -220,22 +218,26 @@ def tile_moe_shf_mlp_silu_kernel(
 
         for e in range(TURNED - 1):
             turn_expert(e)
-        direct_unit(2 * TURNED, banks[3 + TURNED - 1])
-        direct_unit(2 * TURNED + 1, banks[first_ring[(2 * TURNED + 1) % 5]])
+        direct_unit(2 * TURNED, turn_bank[TURNED - 1])
+        direct_unit(2 * TURNED + 1, ring[(2 * TURNED + 1) % len(ring)])
         turn_expert(TURNED - 1)
         for u in range(2 * TURNED + 2, 2 * E):
-            direct_unit(u, banks[first_ring[u % 5]])
-        for e in range(E - 1):
+            direct_unit(u, ring[u % len(ring)])
+
+        behind_turn_of = {0: 1, TURNED: TURNED - 1}
+        for e in range(E):
+            tag = "act_%d" % (2 * behind_turn_of[e] + 1) if e in behind_turn_of else ""
+            h_codes[e] = held([P, C], U32, "h_codes%d" % e, tag)
+        for e in (0, 1, TURNED, TURNED - 1, E - 2):
             quantise(h_codes[e], h_plane[e], grouped[e], 0, C)
         for a in range(2):
             quantise(h_codes[E - 1], h_plane[E - 1], grouped[E - 1], a * P, (a + 1) * P)
 
-        second(0, 0, 512, banks[7], nc.scalar)
-        second(0, 512, 1024, banks[0], nc.scalar)
-        second(0, 1024, 1408, banks[3], nc.vector)
-        second(0, 1408, 1536, banks[4], nc.vector)
+        second(0, 0, BANK, banks[7], nc.scalar)
+        second(0, BANK, 2 * BANK, banks[0], nc.scalar)
+        second(0, 2 * BANK, SLOTS - P, banks[3], nc.vector)
+        second(0, SLOTS - P, SLOTS, banks[4], nc.vector)
 
-        blocks = T // P
         terms = {}
 
         def fetch(j, r, lo=0, hi=T, tag=""):
@@ -264,7 +266,7 @@ def tile_moe_shf_mlp_silu_kernel(
         hs_plane = held([P, T], U8, "hs_plane")
 
         def shared_second(j, bank):
-            for b in range(blocks):
+            for b in range(T // P):
                 nc.tensor.matmul_mx(
                     out=bank[:, b * P : (b + 1) * P], lhsT=hs_codes[:, b * P : (b + 1) * P].bitcast(FP8X4),
                     lhsT_scale=hs_plane[:, b * P : (b + 1) * P], rhs=w2sw[:, j * P : (j + 1) * P].bitcast(FP8X4),
@@ -281,8 +283,8 @@ def tile_moe_shf_mlp_silu_kernel(
             nc.sync.dma_start(out[j * P : (j + 1) * P, :], res[j][:])
 
         def second_tile(j, three):
-            for i in range(3):
-                second(j, i * 512, (i + 1) * 512, banks[three[i]], nc.scalar)
+            for i, b in enumerate(three):
+                second(j, i * BANK, (i + 1) * BANK, banks[b], nc.scalar)
 
         for r in range(TOP):
             fetch(0, r)
@@ -297,43 +299,50 @@ def tile_moe_shf_mlp_silu_kernel(
             fetch(1, r)
         second_tile(2, (1, 7, 0))
         half = T // 2
-        for r in range(TOP - 1):
+        last = TOP - 1
+        for r in range(last):
             fetch(2, r)
-        fetch(2, TOP - 1, 0, half)
+        fetch(2, last, 0, half)
         flip(0, banks[3])
         ys0 = shared_second(0, banks[4])
         second_tile(3, (2, 6, 5))
-        for r in range(TOP - 1):
+        for r in range(last):
             fetch(3, r)
         ys1 = shared_second(1, banks[1])
         finish(0, ys0, banks[7])
         flip(1, banks[0])
-        ys = {2: shared_second(2, banks[3]), 3: shared_second(3, banks[4])}
+        ys_late = {2: shared_second(2, banks[3]), 3: shared_second(3, banks[4])}
         finish(1, ys1, banks[2])
 
         flip_bank = {(2, 0): banks[1], (2, half): banks[7], (3, 0): banks[0], (3, half): banks[2]}
         back_bank = {(2, 0): banks[3], (2, half): banks[6], (3, 0): banks[4], (3, half): banks[5]}
         for j in (2, 3):
             for lo in (half, 0):
-                turn_add(back_bank[j, lo], ys[j], True, False, lo, lo + half)
+                turn_add(back_bank[j, lo], ys_late[j], True, False, lo, lo + half)
+
+        def flip_two_terms(j):
+            for r in range(last):
+                for lo in (half, 0):
+                    turn_add(flip_bank[j, lo], terms[j, r, 0], r == 0, lo == half and r == last - 1, lo, lo + half)
 
         def flip_back(j, lo):
             nc.scalar.copy(flipped[j][:, lo : lo + half], flip_bank[j, lo][:, 0:half])
             turn_add(back_bank[j, lo], flipped[j], False, True, lo, lo + half)
 
-        for j in (2, 3):
-            for r in range(TOP - 1):
-                for lo in (half, 0):
-                    turn_add(flip_bank[j, lo], terms[j, r, 0], r == 0, lo == half and r == TOP - 2, lo, lo + half)
-            if j == 3:
-                fetch(3, TOP - 1, 0, half)
-                fetch(2, TOP - 1, half, T, "gate1")
+        def finish_front(j, queue):
             flip_back(j, half)
-            turn_add(flip_bank[j, 0], terms[j, TOP - 1, 0], False, True, 0, half)
+            turn_add(flip_bank[j, 0], terms[j, last, 0], False, True, 0, half)
             flip_back(j, 0)
             nc.scalar.copy(res[j][:, 0:half], back_bank[j, 0][:, 0:half])
-            nc.sync.dma_start(out[j * P : (j + 1) * P, 0:half], res[j][:, 0:half])
-        fetch(3, TOP - 1, half, T)
+            queue.dma_start(out[j * P : (j + 1) * P, 0:half], res[j][:, 0:half])
+
+        flip_two_terms(2)
+        finish_front(2, nc.sync)
+        flip_two_terms(3)
+        fetch(3, last, 0, half)
+        fetch(2, last, half, T, "gate1")
+        finish_front(3, nc.scalar)
+        fetch(3, last, half, T)
         for j in (2, 3):
-            nc.vector.tensor_tensor(res[j][:, half:T], back_bank[j, half][:, 0:half], terms[j, TOP - 1, half][:], ADD)
+            nc.vector.tensor_tensor(res[j][:, half:T], back_bank[j, half][:, 0:half], terms[j, last, half][:], ADD)
             nc.sync.dma_start(out[j * P : (j + 1) * P, half:T], res[j][:, half:T])

@@ -78,11 +78,11 @@ def tile_moe_shf_mlp_silu_kernel(
             nc.sync.dma_start(tile_ap.bitcast(I32), rows.bitcast(I32))
 
         def load_rows(queue, plane, dram, q):
-            queue.dma_start(plane[32 * q : 32 * q + 4, :], dram[0, 4 * q : 4 * q + 4, :].bitcast(I32))
+            queue.dma_start(plane[q:P:32, :], dram[0, q:16:4, :].bitcast(I32))
 
         def load_expert_rows(queue, plane, dram, q):
-            rows = dram[:, 0, 4 * q : 4 * q + 4, :].rearrange("e r n -> r e n")
-            queue.dma_start(plane[32 * q : 32 * q + 4, :, :], rows.bitcast(I32))
+            rows = dram[:, 0, q:16:4, :].rearrange("e r n -> r e n")
+            queue.dma_start(plane[q:P:32, :, :], rows.bitcast(I32))
 
         load_words(xw, x_words)
         nc.sync.dma_start(offs_sb[:], offs)

@@ -294,28 +294,28 @@ def tile_moe_shf_mlp_silu_kernel(
                 xs[:].bitcast(U8)[:, b * P : (b + 1) * P], shared_words[:].bitcast(FP8X4), shared_plane[:],
             )
         quantise(hs_codes, hs_plane, hs_grouped, 0, T)
-        second_tile(1, (2, 6, 5))
+        second_tile(1, (2, 6, 7))
         for r in range(TOP):
             fetch(1, r)
-        second_tile(2, (1, 7, 0))
+        second_tile(2, (0, 4, 6))
         half = T // 2
         last = TOP - 1
         for r in range(last):
             fetch(2, r)
         fetch(2, last, 0, half)
         flip(0, banks[3])
-        ys0 = shared_second(0, banks[4])
-        second_tile(3, (2, 6, 5))
+        ys0 = shared_second(0, banks[2])
+        second_tile(3, (4, 6, 3))
         for r in range(last):
             fetch(3, r)
-        ys1 = shared_second(1, banks[1])
-        finish(0, ys0, banks[7])
-        flip(1, banks[0])
-        ys_late = {2: shared_second(2, banks[3]), 3: shared_second(3, banks[4])}
-        finish(1, ys1, banks[2])
+        ys1 = shared_second(1, banks[2])
+        finish(0, ys0, banks[0])
+        flip(1, banks[4])
+        ys_late = {2: shared_second(2, banks[3]), 3: shared_second(3, banks[2])}
+        finish(1, ys1, banks[1])
 
-        flip_bank = {(2, 0): banks[1], (2, half): banks[7], (3, 0): banks[0], (3, half): banks[2]}
-        back_bank = {(2, 0): banks[3], (2, half): banks[6], (3, 0): banks[4], (3, half): banks[5]}
+        flip_bank = {(2, 0): banks[0], (2, half): banks[6], (3, 0): banks[6], (3, half): banks[1]}
+        back_bank = {(2, 0): banks[3], (2, half): banks[7], (3, 0): banks[2], (3, half): banks[5]}
         for j in (2, 3):
             for lo in (half, 0):
                 turn_add(back_bank[j, lo], ys_late[j], True, False, lo, lo + half)

from contextlib import ExitStack

import concourse.mybir as mybir
from concourse.masks import make_identity

K, T, E, C, H, N, TOP = 512, 512, 6, 256, 512, 512, 3
SLOTS = E * C
P = 128
BANK = 512
FLOPS = 2 * (SLOTS + T) * (K * H + H * N)

F32 = mybir.dt.float32
BF16 = mybir.dt.bfloat16
I32 = mybir.dt.int32
U32 = mybir.dt.uint32
U16 = mybir.dt.uint16
U8 = mybir.dt.uint8
FP8X4 = mybir.dt.float8_e4m3fn_x4
FP4X4 = mybir.dt.float4_e2m1fn_x4
SILU = mybir.ActivationFunctionType.Silu
MULT = mybir.AluOpType.mult
ADD = mybir.AluOpType.add

TURNED = 3
BYTE_PIECES = (128, 256, 384, 384, 384)
WORD_PIECE = TURNED * C
WINDOW = 1024
W1_LOADS = ((0, 1), (1, TURNED), (TURNED, E))


def tile_moe_shf_mlp_silu_kernel(
    tc, x_words, x_scales, w1_words, w1_scales, w2_words, w2_scales,
    w1s_words, w1s_scales, w2s_words, w2s_scales, gate, offs, pos1, pos2, pos3, out,
):
    nc = tc.nc
    with ExitStack() as ctx:
        keep = ctx.enter_context(tc.tile_pool(name="keep", bufs=1))
        psum = ctx.enter_context(tc.psum_pool(name="psum", bufs=1))

        def held(shape, dtype, name, tag=""):
            return keep.tile(shape, dtype, name=name, tag=tag, align_bytes=64)

        banks = [psum.tile([P, BANK], F32, name="bank%d" % b) for b in range(8)]

        offs_sb = keep.tile([P, SLOTS // 16], U16, name="offs_sb")
        pos_sb = [keep.tile([P, T // 16], U16, name="pos_sb%d" % r) for r in range(TOP)]
        xw_window = held([P, WINDOW], I32, "xw_window")
        xw = xw_window[:, 0:T]
        xs = held([P, T // 4], I32, "xs")
        w1w_load = [held([P, hi - lo, 2 * H], U8, "w1w_load%d" % lo) for lo, hi in W1_LOADS]
        w2w = held([P, E, 2 * N], U8, "w2w")
        w1p = held([P, E, H // 4], I32, "w1p")
        w2p = held([P, E, N // 4], I32, "w2p")
        w1sw = held([P, H], I32, "w1sw")
        w2sw = held([P, N], I32, "w2sw")
        w1sp = held([P, H // 4], I32, "w1sp")
        w2sp = held([P, N // 4], I32, "w2sp")
        gate_sb = [held([P, T], F32, "gate_sb%d" % r, "gate%d" % r) for r in range(TOP)]
        ident = held([P, P], F32, "ident")

        def w1w(e):
            g = max(g for g, (lo, hi) in enumerate(W1_LOADS) if lo <= e)
            return w1w_load[g][:, e - W1_LOADS[g][0], :]

        nc.gpsimd.memset(xs[:], 0)
        nc.vector.memset(w1p[:], 0)
        nc.vector.memset(w1sp[:], 0)
        nc.vector.memset(xw_window[:, T:WINDOW], 0)
        make_identity(nc, ident[:])
        nc.gpsimd.memset(w2p[:], 0)
        nc.gpsimd.memset(w2sp[:], 0)

        def load_words(tile_ap, dram):
            nc.sync.dma_start(tile_ap, dram[0].rearrange("p n d -> p (n d)").bitcast(I32))

        def load_experts(tile_ap, dram, lo, hi):
            rows = dram[lo:hi, 0].rearrange("e p n -> p e n")
            nc.sync.dma_start(tile_ap.bitcast(I32), rows.bitcast(I32))

        def load_rows(queue, plane, dram, q):
            queue.dma_start(plane[q:P:32, :], dram[0, q:16:4, :].bitcast(I32))

        def load_expert_rows(queue, plane, dram, q):
            rows = dram[:, 0, q:16:4, :].rearrange("e r n -> r e n")
            queue.dma_start(plane[q:P:32, :, :], rows.bitcast(I32))

        load_words(xw, x_words)
        nc.sync.dma_start(offs_sb[:], offs)
        for q in range(4):
            load_rows(nc.scalar, xs, x_scales, q)
        load_experts(w1w_load[0][:], w1_words, *W1_LOADS[0])
        for q in range(4):
            load_expert_rows(nc.sync if q < 2 else nc.scalar, w1p, w1_scales, q)
        load_experts(w1w_load[1][:], w1_words, *W1_LOADS[1])
        for q in range(2):
            load_rows(nc.sync, w1sp, w1s_scales, q)
        load_experts(w1w_load[2][:], w1_words, *W1_LOADS[2])
        for q in range(2, 4):
            load_rows(nc.sync, w1sp, w1s_scales, q)
        load_words(w1sw[:], w1s_words)
        load_experts(w2w[:], w2_words, 0, E)
        for q in range(4):
            load_expert_rows(nc.sync, w2p, w2_scales, q)
        for r, pos in enumerate((pos1, pos2, pos3)):
            nc.sync.dma_start(pos_sb[r][:], pos)
            nc.sync.dma_start(gate_sb[r][:], gate[r])
        load_words(w2sw[:], w2s_words)
        for q in range(4):
            load_rows(nc.sync, w2sp, w2s_scales, q)

        def gather(picked, window, at):
            cols = picked.shape[1]
            nc.vector.tensor_copy(picked, window.indirect(offs_sb[:, at // 16 : (at + cols) // 16]))
            return [picked[:, a : a + P] for a in range(0, cols, P)]

        unit_words, unit_plane = [], []
        xg = held([P, WORD_PIECE], U32, "xg")
        unit_words.extend(gather(xg[:], xw_window[:].bitcast(U32), 0))
        for g, cols in enumerate(BYTE_PIECES[:-1]):
            xgp = held([P, cols], U8, "xgp%d" % g, "early%d" % g)
            unit_plane.extend(gather(xgp[:], xs[:].bitcast(U8), sum(BYTE_PIECES[:g])))

        words_by_t = {}
        planes_by_t = held([P, E - TURNED, H], U8, "planes_by_t")
        nc.gpsimd.tensor_copy(
            planes_by_t[:].rearrange("p e (t m) -> p e t m", t=4),
            w1p[:, TURNED:E, :].bitcast(U8).rearrange("p e (m t) -> p e t m", t=4),
        )
        for e in range(TURNED, E):
            words = held([P, H], U16, "w1_words_by_t%d" % e)
            nc.gpsimd.tensor_copy(
                words[:].rearrange("p (t m) -> p t m", t=4), w1w(e).bitcast(U16).rearrange("p (m t) -> p t m", t=4),
            )
            words_by_t[e] = words[:].bitcast(U8)
        shared_words = held([P, H], I32, "w1s_words_by_t")
        shared_plane = held([P, H], U8, "w1s_plane_by_t")
        nc.gpsimd.tensor_copy(
            shared_words[:].rearrange("p (t m) -> p t m", t=4), w1sw[:].rearrange("p (m t) -> p t m", t=4),
        )
        nc.gpsimd.tensor_copy(
            shared_plane[:].rearrange("p (t m) -> p t m", t=4), w1sp[:].bitcast(U8).rearrange("p (m t) -> p t m", t=4),
        )

        def copy_out(engine, dst, src):
            if engine is nc.vector:
                nc.vector.tensor_copy(dst, src)
            else:
                nc.scalar.copy(dst, src)

        def first_turned(u, bank):
            e = u // 2
            nc.tensor.matmul_mx(
                out=bank[:], lhsT=unit_words[u].bitcast(FP8X4), lhsT_scale=unit_plane[u],
                rhs=w1w(e).bitcast(FP4X4), rhs_scale=w1p[:, e, :].bitcast(U8), start=True, stop=True,
            )
            act = held([P, H], BF16, "act_%d" % u, "act_%d" % u)
            nc.scalar.activation(
                act[:].rearrange("s (w p d) -> s w p d", w=2, d=2),
                bank[:].rearrange("s (p w d) -> s w p d", w=2, d=2), SILU,
            )
            return act

        def first_direct(bank, dst, x_codes, x_plane, words, plane):
            for t in range(4):
                nc.tensor.matmul_mx(
                    out=bank[:, t * P : (t + 1) * P], lhsT=words[:, t * P : (t + 1) * P],
                    lhsT_scale=plane[:, t * P : (t + 1) * P], rhs=x_codes.bitcast(FP8X4),
                    rhs_scale=x_plane, start=True, stop=True,
                )
            nc.scalar.activation(
                dst.rearrange("p (s t) -> p s t", t=4), bank[:].rearrange("p (t s) -> p s t", t=4), SILU,
            )

        def quantise(codes, plane, values, lo, hi):
            nc.vector.quantize_mx(out=codes[:, lo:hi].bitcast(FP8X4), scales=plane[:, lo:hi], in_=values[:, 4 * lo : 4 * hi])

        y_sb = [held([P, SLOTS], F32, "y_sb%d" % j) for j in range(N // P)]
        h_codes = {}
        h_plane = [held([P, C], U8, "h_plane%d" % e) for e in range(E)]

        def second(j, lo, hi, bank, engine):
            for e in range(lo // C, (hi + C - 1) // C):
                a, b = max(lo, e * C), min(hi, (e + 1) * C)
                nc.tensor.matmul_mx(
                    out=bank[:, a - lo : b - lo],
                    lhsT=w2w[:, e, 2 * j * P : 2 * (j + 1) * P].bitcast(FP4X4),
                    lhsT_scale=w2p[:, e, :].bitcast(U8)[:, j * P : (j + 1) * P],
                    rhs=h_codes[e][:, a - e * C : b - e * C].bitcast(FP8X4), rhs_scale=h_plane[e][:, a - e * C : b - e * C],
                    start=True, stop=True,
                )
            copy_out(engine, y_sb[j][:, lo:hi], bank[:, 0 : hi - lo])

        grouped = [held([P, 4 * C], BF16, "grouped%d" % e) for e in range(E)]
        ring = [banks[b] for b in (0, 1, 2, 6, 7)]
        turn_bank = banks[3 : 3 + TURNED]
        acts = [first_turned(u, ring[u % len(ring)]) for u in range(2 * TURNED)]
        xg_late = held([P, WORD_PIECE], U32, "xg_late", "early0")
        unit_words.extend(gather(xg_late[:], xw_window[:].bitcast(U32), WORD_PIECE))
        xgp_last = held([P, BYTE_PIECES[-1]], U8, "xgp_last", "early2")
        unit_plane.extend(gather(xgp_last[:], xs[:].bitcast(U8), SLOTS - BYTE_PIECES[-1]))

        def turn_expert(e):
            for a in range(2):
                pairs = acts[2 * e + a][:].bitcast(F32)
                for w in range(2):
                    col = (2 * a + w) * P
                    nc.tensor.transpose(turn_bank[e][:, col : col + P], pairs[:, w * P : (w + 1) * P], ident[:])
            src = turn_bank[e][:].rearrange("p (a w s) -> p a s w", w=2, s=P)
            dst = grouped[e][:].bitcast(F32).rearrange("p (a s w) -> p a s w", w=2, s=P)
            copy_out(nc.scalar if e == 0 else nc.vector, dst, src)

        def direct_unit(u, bank):
            e, a = divmod(u, 2)
            first_direct(
                bank, grouped[e][:, a * H : (a + 1) * H], unit_words[u], unit_plane[u],
                words_by_t[e].bitcast(FP4X4), planes_by_t[:, e - TURNED, :],
            )

        for e in range(TURNED - 1):
            turn_expert(e)
        direct_unit(2 * TURNED, turn_bank[TURNED - 1])
        direct_unit(2 * TURNED + 1, ring[(2 * TURNED + 1) % len(ring)])
        turn_expert(TURNED - 1)
        for u in range(2 * TURNED + 2, 2 * E):
            direct_unit(u, ring[u % len(ring)])

        behind_turn_of = {0: 1, TURNED: TURNED - 1}
        for e in range(E):
            tag = "act_%d" % (2 * behind_turn_of[e] + 1) if e in behind_turn_of else ""
            h_codes[e] = held([P, C], U32, "h_codes%d" % e, tag)
        for e in (0, 1, TURNED, TURNED - 1, E - 2):
            quantise(h_codes[e], h_plane[e], grouped[e], 0, C)
        for a in range(2):
            quantise(h_codes[E - 1], h_plane[E - 1], grouped[E - 1], a * P, (a + 1) * P)

        second(0, 0, BANK, banks[7], nc.scalar)
        second(0, BANK, 2 * BANK, banks[0], nc.scalar)
        second(0, 2 * BANK, SLOTS - P, banks[3], nc.vector)
        second(0, SLOTS - P, SLOTS, banks[4], nc.vector)

        terms = {}

        def fetch(j, r, lo=0, hi=T, tag=""):
            term = held([P, hi - lo], F32, "term%d_%d_%d" % (j, r, lo), tag)
            picks = pos_sb[r][:, lo // 16 : hi // 16]
            nc.vector.tensor_tensor(term[:], y_sb[j][:].indirect(picks), gate_sb[r][:, lo:hi], MULT)
            terms[j, r, lo] = term

        def turn_add(bank, source, opens, closes, lo=0, hi=T):
            for at in range(lo, hi, P):
                nc.tensor.matmul(
                    bank[:, at - lo : at - lo + P], lhsT=source[:, at : at + P], rhs=ident[:],
                    start=(opens and at == lo), stop=(closes and at + P == hi), is_transpose=True,
                )

        flipped = [held([P, T], F32, "flipped%d" % j) for j in range(N // P)]
        res = [held([P, T], F32, "res%d" % j) for j in range(N // P)]

        def flip(j, bank):
            for r in range(TOP):
                turn_add(bank, terms[j, r, 0], r == 0, r == TOP - 1)
            nc.scalar.copy(flipped[j][:], bank[:])

        hs_grouped = held([P, 4 * T], BF16, "hs_grouped")
        hs_codes = held([P, T], U32, "hs_codes")
        hs_plane = held([P, T], U8, "hs_plane")

        def shared_second(j, bank):
            for b in range(T // P):
                nc.tensor.matmul_mx(
                    out=bank[:, b * P : (b + 1) * P], lhsT=hs_codes[:, b * P : (b + 1) * P].bitcast(FP8X4),
                    lhsT_scale=hs_plane[:, b * P : (b + 1) * P], rhs=w2sw[:, j * P : (j + 1) * P].bitcast(FP8X4),
                    rhs_scale=w2sp[:].bitcast(U8)[:, j * P : (j + 1) * P], start=True, stop=True,
                )
            ys = held([P, T], F32, "ys%d" % j)
            nc.scalar.copy(ys[:], bank[:])
            return ys

        def finish(j, ys, bank):
            turn_add(bank, ys, True, False)
            turn_add(bank, flipped[j], False, True)
            nc.scalar.copy(res[j][:], bank[:])
            nc.sync.dma_start(out[j * P : (j + 1) * P, :], res[j][:])

        def second_tile(j, three):
            for i, b in enumerate(three):
                second(j, i * BANK, (i + 1) * BANK, banks[b], nc.scalar)

        for r in range(TOP):
            fetch(0, r)
        for b, bank in enumerate((7, 0, 3, 4)):
            first_direct(
                banks[bank], hs_grouped[:, b * H : (b + 1) * H], xw[:, b * P : (b + 1) * P],
                xs[:].bitcast(U8)[:, b * P : (b + 1) * P], shared_words[:].bitcast(FP8X4), shared_plane[:],
            )
        quantise(hs_codes, hs_plane, hs_grouped, 0, T)
        second_tile(1, (2, 6, 7))
        for r in range(TOP):
            fetch(1, r)
        second_tile(2, (0, 4, 6))
        half = T // 2
        last = TOP - 1
        for r in range(last):
            fetch(2, r)
        fetch(2, last, 0, half)
        flip(0, banks[3])
        ys0 = shared_second(0, banks[2])
        second_tile(3, (4, 6, 3))
        for r in range(last):
            fetch(3, r)
        ys1 = shared_second(1, banks[2])
        finish(0, ys0, banks[0])
        flip(1, banks[4])
        ys_late = {2: shared_second(2, banks[3]), 3: shared_second(3, banks[2])}
        finish(1, ys1, banks[1])

        flip_bank = {(2, 0): banks[0], (2, half): banks[6], (3, 0): banks[6], (3, half): banks[1]}
        back_bank = {(2, 0): banks[3], (2, half): banks[7], (3, 0): banks[2], (3, half): banks[5]}
        for j in (2, 3):
            for lo in (half, 0):
                turn_add(back_bank[j, lo], ys_late[j], True, False, lo, lo + half)

        def flip_two_terms(j):
            for r in range(last):
                for lo in (half, 0):
                    turn_add(flip_bank[j, lo], terms[j, r, 0], r == 0, lo == half and r == last - 1, lo, lo + half)

        def flip_back(j, lo):
            nc.scalar.copy(flipped[j][:, lo : lo + half], flip_bank[j, lo][:, 0:half])
            turn_add(back_bank[j, lo], flipped[j], False, True, lo, lo + half)

        def finish_front(j, queue):
            flip_back(j, half)
            turn_add(flip_bank[j, 0], terms[j, last, 0], False, True, 0, half)
            flip_back(j, 0)
            nc.scalar.copy(res[j][:, 0:half], back_bank[j, 0][:, 0:half])
            queue.dma_start(out[j * P : (j + 1) * P, 0:half], res[j][:, 0:half])

        flip_two_terms(2)
        finish_front(2, nc.sync)
        flip_two_terms(3)
        fetch(3, last, 0, half)
        fetch(2, last, half, T, "gate1")
        finish_front(3, nc.scalar)
        fetch(3, last, half, T)
        for j in (2, 3):
            nc.vector.tensor_tensor(res[j][:, half:T], back_bank[j, half][:, 0:half], terms[j, last, half][:], ADD)
            nc.sync.dma_start(out[j * P : (j + 1) * P, half:T], res[j][:, half:T])
